import numpy as np
import ml_dtypes


def mxq(x, axis, fmt="e4m3"):
    dtype, down = {"e4m3": (ml_dtypes.float8_e4m3fn, 7), "e5m2": (ml_dtypes.float8_e5m2, 14)}[fmt]
    v = np.moveaxis(np.asarray(x, np.float32).astype(ml_dtypes.bfloat16).astype(np.float64), axis, -1)
    blocks = v.reshape(v.shape[:-1] + (-1, 32))
    amax = np.abs(blocks).max(-1, keepdims=True)
    byte = np.maximum(np.where(amax > 0, np.frexp(amax)[1] - 1 + 127, 0) - down, 1)
    scale = np.exp2(byte - 127.0)
    codes = (blocks / scale).astype(np.float32).astype(dtype).astype(np.float64)
    return np.moveaxis((codes * scale).reshape(v.shape), -1, axis)


WIDE = False


def mx_kscale(k):
    if not WIDE:
        return np.ones(k)
    levels = np.array([10, -10, 5, -5, 0])
    if k % 512:
        return np.exp2(np.random.permutation(np.resize(levels, k // 32))).repeat(32)
    a = np.empty((k // 512, 16))
    for p in range(k // 512):
        a[p, :8] = np.random.permutation(np.resize(levels, 8))
        for g in range(8):
            far = levels[np.abs(levels - a[p, g]) >= 10]
            a[p, g + 8] = far[np.random.randint(len(far))]
    return np.exp2(a.ravel()).repeat(32)


def f64(x):
    return np.asarray(x).astype(np.float64)


E2M1 = np.array([0.0, 0.5, 1.0, 1.5, 2.0, 3.0, 4.0, 6.0, -0.0, -0.5, -1.0, -1.5, -2.0, -3.0, -4.0, -6.0])


def pack_weight(w, fmt):
    k, n = w.shape
    w = f64(np.asarray(w, np.float32).astype(ml_dtypes.bfloat16)).reshape(k // 32, 32, n)
    amax = np.abs(w).max(1)
    if fmt == "e4m3":
        byte = np.frexp(amax)[1] - 1 + 127 - 7
    else:
        mant, ex = np.frexp(amax / 6.0)
        byte = np.where(mant > 0.5, ex, ex - 1) + 127
    byte = np.clip(np.where(amax > 0, byte, 1), 1, 254)
    scaled = (w * np.exp2(127.0 - byte)[:, None, :]).reshape(k, n).astype(np.float32)
    by_word = np.ascontiguousarray(scaled.reshape(k // 512, 128, 4, n).transpose(0, 1, 3, 2))
    if fmt == "e4m3":
        words = by_word.astype(ml_dtypes.float8_e4m3fn).view(np.uint8)
    else:
        c = by_word.astype(ml_dtypes.float4_e2m1fn).view(np.uint8) & 0xF
        words = (c[..., 0::2] | (c[..., 1::2] << 4)).reshape(k // 512, 128, 2 * n)
    return np.ascontiguousarray(words), np.ascontiguousarray(byte.astype(np.uint8).reshape(k // 512, 16, n))


def unpack_weight(words, scales, fmt):
    g, _, n = scales.shape
    words = np.ascontiguousarray(words).reshape(g, 128, n, -1)
    if fmt == "e4m3":
        vals = words.view(ml_dtypes.float8_e4m3fn).astype(np.float64)
    else:
        nib = np.empty((g, 128, n, 4), np.uint8)
        nib[..., 0::2] = words & 0xF
        nib[..., 1::2] = words >> 4
        vals = E2M1[nib]
    vals = vals * np.repeat(np.exp2(scales.astype(np.float64) - 127.0), 8, axis=1)[..., None]
    return vals.transpose(0, 1, 3, 2).reshape(g * 512, n)


K, M, T = 2048, 1024, 512


def setup_inputs():
    n = np.random.standard_normal
    s = mx_kscale(K)[:, None]
    x = n((K, T)) * s
    x4 = pack_weight(x, "e2m1")
    rest = x - unpack_weight(*x4, "e2m1")
    p_w4 = pack_weight(n((K, M)) / np.sqrt(K) / s, "e2m1")
    return {
        "x4_words": x4[0],
        "x4_scales": x4[1],
        "xr": (rest).astype(np.float32),
        "w4_words": p_w4[0],
        "w4_scales": p_w4[1],
        "g": (n((512, 1024))).astype(np.float32),
    }


def reference(x4_words, x4_scales, xr, w4_words, w4_scales, g):
    x4_ = unpack_weight(x4_words, x4_scales, "e2m1")
    xr_ = mxq(f64(xr), 0, "e4m3")
    w4_ = unpack_weight(w4_words, w4_scales, "e2m1")
    y = x4_.T @ w4_ + xr_.T @ w4_
    return f64(g) * y

@@ -1,0 +1,193 @@
+from contextlib import ExitStack
+
+import concourse.mybir as mybir
+
+K, N, T = 2048, 1024, 512
+FLOPS = 2 * 2 * K * N * T
+
+F32 = mybir.dt.float32
+BF16 = mybir.dt.bfloat16
+U32 = mybir.dt.uint32
+I32 = mybir.dt.int32
+U8 = mybir.dt.uint8
+FP8X4 = mybir.dt.float8_e4m3fn_x4
+FP4X4 = mybir.dt.float4_e2m1fn_x4
+
+P = 128
+A = K // 512
+TT = T // P
+NH = 2
+HALF = N // NH
+VCOLS = 256
+FIRST = 2
+EARLY = 2
+
+
+def tile_mix_xres_tm_mul_kernel(tc, x4_words, x4_scales, xr, w4_words, w4_scales, g, out):
+    nc = tc.nc
+    with ExitStack() as ctx:
+        keep = ctx.enter_context(tc.tile_pool(name="keep", bufs=1))
+        psum = ctx.enter_context(tc.psum_pool(name="psum", bufs=1))
+        ctx.enter_context(tc.manual_schedule())
+
+        x0 = keep.tile([P, 1, 2 * T], U8, name="x0", align_bytes=256)
+        x123 = keep.tile([P, A - 1, 2 * T], U8, name="x123", align_bytes=256)
+        w0 = keep.tile([P, 1, 2 * N], U8, name="w0", align_bytes=256)
+        w1 = keep.tile([P, 1, 2 * N], U8, name="w1", align_bytes=256)
+        w23 = keep.tile([P, 2, 2 * N], U8, name="w23", align_bytes=256)
+        xs = keep.tile([P, A, T], U8, name="xs", align_bytes=256)
+        ws = keep.tile([P, A, N], U8, name="ws", align_bytes=256)
+        dummy = keep.tile([P, 8], F32, name="dummy")
+        dummy_out = keep.tile([P, 8], F32, name="dummy_out")
+
+        def flat_i32(t):
+            return t[:].rearrange("p a n -> p (a n)").bitcast(I32)
+
+        nc.vector.memset(flat_i32(ws), 0)
+        nc.vector.memset(flat_i32(xs), 0)
+        nc.vector.memset(dummy[:], 0.0)
+
+        def load_scales(engine, tile, dram, r):
+            n4 = dram.shape[2] // 4
+            engine.dma_start(
+                out=flat_i32(tile)[r:P:32, :].rearrange("q (a n) -> q a n", n=n4),
+                in_=dram.bitcast(I32)[:, r:16:4, :].rearrange("a q n -> q a n"),
+            )
+
+        raw = []
+        for a, widths in enumerate(((VCOLS, T - VCOLS), (T,), (T,), (T,))):
+            pieces, t0 = [], 0
+            for width in widths:
+                piece = keep.tile([P, 4, width], F32, name="raw%d_%d" % (a, t0), align_bytes=256)
+                pieces.append((t0, t0 + width, piece))
+                t0 += width
+            raw.append(pieces)
+
+        def load_raw(a, i):
+            t0, t1, piece = raw[a][i]
+            nc.sync.dma_start(
+                out=piece[:], in_=xr[512 * a : 512 * (a + 1), t0:t1].rearrange("(p j) t -> p j t", j=4)
+            )
+
+        load_raw(0, 0)
+        nc.sync.dma_start(out=w0[:, 0, :], in_=w4_words[0])
+        for r in range(4):
+            load_scales(nc.sync, ws, w4_scales, r)
+        nc.sync.dma_start(out=x0[:, 0, :], in_=x4_words[0])
+        for r in range(4):
+            load_scales(nc.sync, xs, x4_scales, r)
+        nc.sync.dma_start(out=w1[:, 0, :], in_=w4_words[1])
+        nc.sync.dma_start(out=x123[:], in_=x4_words[1:A].rearrange("a p n -> p a n"))
+        nc.sync.dma_start(out=w23[:], in_=w4_words[2:A].rearrange("a p n -> p a n"))
+        nc.scalar.copy(dummy_out[:], dummy[:])
+        load_raw(0, 1)
+        for a in range(1, A):
+            load_raw(a, 0)
+        g_sb = []
+        for t in range(TT):
+            g_t = keep.tile([P, N], F32, name="g%d" % t, align_bytes=256)
+            nc.sync.dma_start(out=g_t[:], in_=g[P * t : P * (t + 1), :])
+            g_sb.append(g_t)
+
+        banks = []
+        for i in range(TT * NH):
+            bank = psum.tile([P, HALF], F32, name="bank%d" % i)
+            banks.append(bank)
+
+        def w_operand(a, h):
+            words, b = ((w0, 0), (w1, 0), (w23, 0), (w23, 1))[a]
+            return (
+                words[:, b, 2 * HALF * h : 2 * HALF * (h + 1)].bitcast(FP4X4),
+                ws[:, a, HALF * h : HALF * (h + 1)],
+            )
+
+        def x4_pass(a, t, h):
+            words, b = (x0, 0) if a == 0 else (x123, a - 1)
+            rhs, rhs_scale = w_operand(a, h)
+            nc.tensor.matmul_mx(
+                out=banks[NH * t + h][:],
+                lhsT=words[:, b, 2 * P * t : 2 * P * (t + 1)].bitcast(FP4X4),
+                lhsT_scale=xs[:, a, P * t : P * (t + 1)],
+                rhs=rhs,
+                rhs_scale=rhs_scale,
+                start=(a == 0 and t >= FIRST),
+                stop=False,
+            )
+
+        xb, codes, scales = [], [], []
+        for a in range(A):
+            xb_a = keep.tile([P, T, 4], BF16, name="xb%d" % a, align_bytes=256)
+            c_a = keep.tile([P, T], U32, name="codes%d" % a, align_bytes=256)
+            s_a = keep.tile([P, T], U8, name="scales%d" % a, align_bytes=256)
+            xb.append(xb_a)
+            codes.append(c_a)
+            scales.append(s_a)
+
+        def interleave(copy, a, t0, t1):
+            for p0, p1, piece in raw[a]:
+                if p0 <= t0 and t1 <= p1:
+                    copy(xb[a][:, t0:t1, :], piece[:, :, t0 - p0 : t1 - p0].rearrange("p j t -> p t j"))
+
+        def quantize(a, t0, t1):
+            nc.vector.quantize_mx(
+                out=codes[a][:, t0:t1].bitcast(FP8X4),
+                scales=scales[a][:, t0:t1],
+                in_=xb[a][:, t0:t1, :].rearrange("p t j -> p (t j)"),
+            )
+
+        def xr_pass(a, t, h):
+            rhs, rhs_scale = w_operand(a, h)
+            nc.tensor.matmul_mx(
+                out=banks[NH * t + h][:],
+                lhsT=codes[a][:, P * t : P * (t + 1)].bitcast(FP8X4),
+                lhsT_scale=scales[a][:, P * t : P * (t + 1)],
+                rhs=rhs,
+                rhs_scale=rhs_scale,
+                start=(a == 0 and t < FIRST),
+                stop=(a == A - 1),
+            )
+
+        for t, copy in enumerate((nc.vector.tensor_copy, nc.scalar.copy)):
+            interleave(copy, 0, P * t, P * (t + 1))
+            quantize(0, P * t, P * (t + 1))
+            for h in range(NH):
+                xr_pass(0, t, h)
+
+        for a in range(A):
+            for h in range(NH):
+                for t in range(TT):
+                    x4_pass(a, t, h)
+
+        for a in range(A):
+            if a > 0:
+                interleave(nc.vector.tensor_copy, a, 0, VCOLS)
+            interleave(nc.scalar.copy, a, VCOLS, T)
+            if a > 0:
+                quantize(a, 0, VCOLS)
+            quantize(a, VCOLS, T)
+
+        for a, tiles in ((0, range(FIRST, TT)), (1, range(EARLY))):
+            for t in tiles:
+                for h in range(NH):
+                    xr_pass(a, t, h)
+
+        for t in range(TT):
+            result = keep.tile([P, N], F32, name="result%d" % t, align_bytes=256)
+            rows = slice(P * t, P * (t + 1))
+            for h in range(NH):
+                for a in range(2 if t < EARLY else 1, A):
+                    xr_pass(a, t, h)
+                parts = 2 if (t, h) == (TT - 1, NH - 1) else 1
+                for j in range(parts):
+                    b_cols = slice(HALF // parts * j, HALF // parts * (j + 1))
+                    cols = slice(HALF * h + b_cols.start, HALF * h + b_cols.stop)
+                    nc.vector.tensor_tensor(
+                        out=result[:, cols],
+                        in0=banks[NH * t + h][:, b_cols],
+                        in1=g_sb[t][:, cols],
+                        op=mybir.AluOpType.mult,
+                    )
+                    if t == TT - 1:
+                        nc.sync.dma_start(out=out[rows, cols], in_=result[:, cols])
+            if t < TT - 1:
+                nc.sync.dma_start(out=out[rows, :], in_=result[:])

@@ -19,7 +19,6 @@ TT = T // P
 NH = 2
 HALF = N // NH
 VCOLS = 256
-FIRST = 2
 EARLY = 2
 
 
@@ -30,32 +29,29 @@ def tile_mix_xres_tm_mul_kernel(tc, x4_words, x4_scales, xr, w4_words, w4_scales
         psum = ctx.enter_context(tc.psum_pool(name="psum", bufs=1))
         ctx.enter_context(tc.manual_schedule())
 
-        x0 = keep.tile([P, 1, 2 * T], U8, name="x0", align_bytes=256)
-        x123 = keep.tile([P, A - 1, 2 * T], U8, name="x123", align_bytes=256)
+        xw = keep.tile([P, A, 2 * T], U8, name="xw", align_bytes=256)
         w0 = keep.tile([P, 1, 2 * N], U8, name="w0", align_bytes=256)
-        w1 = keep.tile([P, 1, 2 * N], U8, name="w1", align_bytes=256)
-        w23 = keep.tile([P, 2, 2 * N], U8, name="w23", align_bytes=256)
+        w123 = keep.tile([P, A - 1, 2 * N], U8, name="w123", align_bytes=256)
         xs = keep.tile([P, A, T], U8, name="xs", align_bytes=256)
-        ws = keep.tile([P, A, N], U8, name="ws", align_bytes=256)
-        dummy = keep.tile([P, 8], F32, name="dummy")
-        dummy_out = keep.tile([P, 8], F32, name="dummy_out")
+        ws0 = keep.tile([P, 1, N], U8, name="ws0", align_bytes=256)
+        ws123 = keep.tile([P, A - 1, N], U8, name="ws123", align_bytes=256)
 
         def flat_i32(t):
             return t[:].rearrange("p a n -> p (a n)").bitcast(I32)
 
-        nc.vector.memset(flat_i32(ws), 0)
-        nc.vector.memset(flat_i32(xs), 0)
-        nc.vector.memset(dummy[:], 0.0)
+        for plane in (ws0, xs, ws123):
+            nc.vector.memset(flat_i32(plane), 0)
 
-        def load_scales(engine, tile, dram, r):
+        def load_scales(tile, dram, a0, a1):
             n4 = dram.shape[2] // 4
-            engine.dma_start(
-                out=flat_i32(tile)[r:P:32, :].rearrange("q (a n) -> q a n", n=n4),
-                in_=dram.bitcast(I32)[:, r:16:4, :].rearrange("a q n -> q a n"),
-            )
+            for r in range(4):
+                nc.sync.dma_start(
+                    out=flat_i32(tile)[r:P:32, :].rearrange("q (a n) -> q a n", n=n4),
+                    in_=dram.bitcast(I32)[a0:a1, r:16:4, :].rearrange("a q n -> q a n"),
+                )
 
         raw = []
-        for a, widths in enumerate(((VCOLS, T - VCOLS), (T,), (T,), (T,))):
+        for a, widths in enumerate(((P, T - P), (T,), (T,), (T,))):
             pieces, t0 = [], 0
             for width in widths:
                 piece = keep.tile([P, 4, width], F32, name="raw%d_%d" % (a, t0), align_bytes=256)
@@ -70,24 +66,20 @@ def tile_mix_xres_tm_mul_kernel(tc, x4_words, x4_scales, xr, w4_words, w4_scales
             )
 
         load_raw(0, 0)
+        load_scales(ws0, w4_scales, 0, 1)
         nc.sync.dma_start(out=w0[:, 0, :], in_=w4_words[0])
-        for r in range(4):
-            load_scales(nc.sync, ws, w4_scales, r)
-        nc.sync.dma_start(out=x0[:, 0, :], in_=x4_words[0])
-        for r in range(4):
-            load_scales(nc.sync, xs, x4_scales, r)
-        nc.sync.dma_start(out=w1[:, 0, :], in_=w4_words[1])
-        nc.sync.dma_start(out=x123[:], in_=x4_words[1:A].rearrange("a p n -> p a n"))
-        nc.sync.dma_start(out=w23[:], in_=w4_words[2:A].rearrange("a p n -> p a n"))
-        nc.scalar.copy(dummy_out[:], dummy[:])
+        nc.sync.dma_start(out=xw[:], in_=x4_words.rearrange("a p n -> p a n"))
+        load_scales(xs, x4_scales, 0, A)
         load_raw(0, 1)
+        nc.sync.dma_start(out=w123[:], in_=w4_words[1:A].rearrange("a p n -> p a n"))
+        load_scales(ws123, w4_scales, 1, A)
         for a in range(1, A):
             load_raw(a, 0)
         g_sb = []
-        for t in range(TT):
-            g_t = keep.tile([P, N], F32, name="g%d" % t, align_bytes=256)
-            nc.sync.dma_start(out=g_t[:], in_=g[P * t : P * (t + 1), :])
-            g_sb.append(g_t)
+        for u in range(TT // 2):
+            g_u = keep.tile([P, 2, N], F32, name="g%d" % u, align_bytes=256)
+            nc.sync.dma_start(out=g_u[:], in_=g[2 * P * u : 2 * P * (u + 1), :].rearrange("(b p) n -> p b n", p=P))
+            g_sb.append(g_u)
 
         banks = []
         for i in range(TT * NH):
@@ -95,22 +87,21 @@ def tile_mix_xres_tm_mul_kernel(tc, x4_words, x4_scales, xr, w4_words, w4_scales
             banks.append(bank)
 
         def w_operand(a, h):
-            words, b = ((w0, 0), (w1, 0), (w23, 0), (w23, 1))[a]
+            words, plane, c = (w0, ws0, 0) if a == 0 else (w123, ws123, a - 1)
             return (
-                words[:, b, 2 * HALF * h : 2 * HALF * (h + 1)].bitcast(FP4X4),
-                ws[:, a, HALF * h : HALF * (h + 1)],
+                words[:, c, 2 * HALF * h : 2 * HALF * (h + 1)].bitcast(FP4X4),
+                plane[:, c, HALF * h : HALF * (h + 1)],
             )
 
         def x4_pass(a, t, h):
-            words, b = (x0, 0) if a == 0 else (x123, a - 1)
             rhs, rhs_scale = w_operand(a, h)
             nc.tensor.matmul_mx(
                 out=banks[NH * t + h][:],
-                lhsT=words[:, b, 2 * P * t : 2 * P * (t + 1)].bitcast(FP4X4),
+                lhsT=xw[:, a, 2 * P * t : 2 * P * (t + 1)].bitcast(FP4X4),
                 lhsT_scale=xs[:, a, P * t : P * (t + 1)],
                 rhs=rhs,
                 rhs_scale=rhs_scale,
-                start=(a == 0 and t >= FIRST),
+                start=(a == 0 and t > 0),
                 stop=False,
             )
 
@@ -126,7 +117,10 @@ def tile_mix_xres_tm_mul_kernel(tc, x4_words, x4_scales, xr, w4_words, w4_scales
         def interleave(copy, a, t0, t1):
             for p0, p1, piece in raw[a]:
                 if p0 <= t0 and t1 <= p1:
-                    copy(xb[a][:, t0:t1, :], piece[:, :, t0 - p0 : t1 - p0].rearrange("p j t -> p t j"))
+                    copy(
+                        xb[a][:, t0:t1, :].rearrange("p (c i) j -> p c j i", i=4),
+                        piece[:, :, t0 - p0 : t1 - p0].rearrange("p j (c i) -> p c j i", i=4),
+                    )
 
         def quantize(a, t0, t1):
             nc.vector.quantize_mx(
@@ -143,31 +137,33 @@ def tile_mix_xres_tm_mul_kernel(tc, x4_words, x4_scales, xr, w4_words, w4_scales
                 lhsT_scale=scales[a][:, P * t : P * (t + 1)],
                 rhs=rhs,
                 rhs_scale=rhs_scale,
-                start=(a == 0 and t < FIRST),
+                start=(a == 0 and t == 0),
                 stop=(a == A - 1),
             )
 
-        for t, copy in enumerate((nc.vector.tensor_copy, nc.scalar.copy)):
-            interleave(copy, 0, P * t, P * (t + 1))
-            quantize(0, P * t, P * (t + 1))
+        interleave(nc.vector.tensor_copy, 0, 0, P)
+        quantize(0, 0, P)
+        for a in range(A):
+            v0 = P if a == 0 else 0
+            interleave(nc.vector.tensor_copy, a, v0, VCOLS)
+            interleave(nc.scalar.copy, a, VCOLS, T)
+            quantize(a, v0, VCOLS)
+            quantize(a, VCOLS, T)
+
+        for h in range(NH):
+            xr_pass(0, 0, h)
+        for h in range(NH):
+            for t in range(TT):
+                x4_pass(0, t, h)
+        for t in range(1, TT):
             for h in range(NH):
                 xr_pass(0, t, h)
-
-        for a in range(A):
+        for a in range(1, A):
             for h in range(NH):
                 for t in range(TT):
                     x4_pass(a, t, h)
-
-        for a in range(A):
-            if a > 0:
-                interleave(nc.vector.tensor_copy, a, 0, VCOLS)
-            interleave(nc.scalar.copy, a, VCOLS, T)
-            if a > 0:
-                quantize(a, 0, VCOLS)
-            quantize(a, VCOLS, T)
-
-        for a, tiles in ((0, range(FIRST, TT)), (1, range(EARLY))):
-            for t in tiles:
+        for a in range(1, A - 1):
+            for t in range(EARLY):
                 for h in range(NH):
                     xr_pass(a, t, h)
 
@@ -175,7 +171,7 @@ def tile_mix_xres_tm_mul_kernel(tc, x4_words, x4_scales, xr, w4_words, w4_scales
             result = keep.tile([P, N], F32, name="result%d" % t, align_bytes=256)
             rows = slice(P * t, P * (t + 1))
             for h in range(NH):
-                for a in range(2 if t < EARLY else 1, A):
+                for a in range(A - 1 if t < EARLY else 1, A):
                     xr_pass(a, t, h)
                 parts = 2 if (t, h) == (TT - 1, NH - 1) else 1
                 for j in range(parts):
@@ -184,7 +180,7 @@ def tile_mix_xres_tm_mul_kernel(tc, x4_words, x4_scales, xr, w4_words, w4_scales
                     nc.vector.tensor_tensor(
                         out=result[:, cols],
                         in0=banks[NH * t + h][:, b_cols],
-                        in1=g_sb[t][:, cols],
+                        in1=g_sb[t // 2][:, t % 2, cols],
                         op=mybir.AluOpType.mult,
                     )
                     if t == TT - 1:

@@ -29,9 +29,11 @@ def tile_mix_xres_tm_mul_kernel(tc, x4_words, x4_scales, xr, w4_words, w4_scales
         psum = ctx.enter_context(tc.psum_pool(name="psum", bufs=1))
         ctx.enter_context(tc.manual_schedule())
 
-        xw = keep.tile([P, A, 2 * T], U8, name="xw", align_bytes=256)
+        x0 = keep.tile([P, 1, 2 * T], U8, name="x0", align_bytes=256)
+        x123 = keep.tile([P, A - 1, 2 * T], U8, name="x123", align_bytes=256)
         w0 = keep.tile([P, 1, 2 * N], U8, name="w0", align_bytes=256)
-        w123 = keep.tile([P, A - 1, 2 * N], U8, name="w123", align_bytes=256)
+        w1 = keep.tile([P, 1, 2 * N], U8, name="w1", align_bytes=256)
+        w23 = keep.tile([P, 2, 2 * N], U8, name="w23", align_bytes=256)
         xs = keep.tile([P, A, T], U8, name="xs", align_bytes=256)
         ws0 = keep.tile([P, 1, N], U8, name="ws0", align_bytes=256)
         ws123 = keep.tile([P, A - 1, N], U8, name="ws123", align_bytes=256)
@@ -42,10 +44,10 @@ def tile_mix_xres_tm_mul_kernel(tc, x4_words, x4_scales, xr, w4_words, w4_scales
         for plane in (ws0, xs, ws123):
             nc.vector.memset(flat_i32(plane), 0)
 
-        def load_scales(tile, dram, a0, a1):
+        def load_scales(queue, tile, dram, a0, a1):
             n4 = dram.shape[2] // 4
             for r in range(4):
-                nc.sync.dma_start(
+                queue.dma_start(
                     out=flat_i32(tile)[r:P:32, :].rearrange("q (a n) -> q a n", n=n4),
                     in_=dram.bitcast(I32)[a0:a1, r:16:4, :].rearrange("a q n -> q a n"),
                 )
@@ -66,13 +68,15 @@ def tile_mix_xres_tm_mul_kernel(tc, x4_words, x4_scales, xr, w4_words, w4_scales
             )
 
         load_raw(0, 0)
-        load_scales(ws0, w4_scales, 0, 1)
+        load_scales(nc.sync, ws0, w4_scales, 0, 1)
         nc.sync.dma_start(out=w0[:, 0, :], in_=w4_words[0])
-        nc.sync.dma_start(out=xw[:], in_=x4_words.rearrange("a p n -> p a n"))
-        load_scales(xs, x4_scales, 0, A)
+        nc.sync.dma_start(out=x0[:, 0, :], in_=x4_words[0])
+        load_scales(nc.sync, xs, x4_scales, 0, A)
         load_raw(0, 1)
-        nc.sync.dma_start(out=w123[:], in_=w4_words[1:A].rearrange("a p n -> p a n"))
-        load_scales(ws123, w4_scales, 1, A)
+        load_scales(nc.gpsimd, ws123, w4_scales, 1, A)
+        nc.sync.dma_start(out=w1[:, 0, :], in_=w4_words[1])
+        nc.sync.dma_start(out=x123[:], in_=x4_words[1:A].rearrange("a p n -> p a n"))
+        nc.sync.dma_start(out=w23[:], in_=w4_words[2:A].rearrange("a p n -> p a n"))
         for a in range(1, A):
             load_raw(a, 0)
         g_sb = []
@@ -87,17 +91,19 @@ def tile_mix_xres_tm_mul_kernel(tc, x4_words, x4_scales, xr, w4_words, w4_scales
             banks.append(bank)
 
         def w_operand(a, h):
-            words, plane, c = (w0, ws0, 0) if a == 0 else (w123, ws123, a - 1)
+            words, b = ((w0, 0), (w1, 0), (w23, 0), (w23, 1))[a]
+            plane, c = (ws0, 0) if a == 0 else (ws123, a - 1)
             return (
-                words[:, c, 2 * HALF * h : 2 * HALF * (h + 1)].bitcast(FP4X4),
+                words[:, b, 2 * HALF * h : 2 * HALF * (h + 1)].bitcast(FP4X4),
                 plane[:, c, HALF * h : HALF * (h + 1)],
             )
 
         def x4_pass(a, t, h):
+            words, b = (x0, 0) if a == 0 else (x123, a - 1)
             rhs, rhs_scale = w_operand(a, h)
             nc.tensor.matmul_mx(
                 out=banks[NH * t + h][:],
-                lhsT=xw[:, a, 2 * P * t : 2 * P * (t + 1)].bitcast(FP4X4),
+                lhsT=words[:, b, 2 * P * t : 2 * P * (t + 1)].bitcast(FP4X4),
                 lhsT_scale=xs[:, a, P * t : P * (t + 1)],
                 rhs=rhs,
                 rhs_scale=rhs_scale,

@@ -19,7 +19,6 @@ TT = T // P
 NH = 2
 HALF = N // NH
 VCOLS = 256
-EARLY = 2
 
 
 def tile_mix_xres_tm_mul_kernel(tc, x4_words, x4_scales, xr, w4_words, w4_scales, g, out):
@@ -29,11 +28,13 @@ def tile_mix_xres_tm_mul_kernel(tc, x4_words, x4_scales, xr, w4_words, w4_scales
         psum = ctx.enter_context(tc.psum_pool(name="psum", bufs=1))
         ctx.enter_context(tc.manual_schedule())
 
-        x0 = keep.tile([P, 1, 2 * T], U8, name="x0", align_bytes=256)
-        x123 = keep.tile([P, A - 1, 2 * T], U8, name="x123", align_bytes=256)
-        w0 = keep.tile([P, 1, 2 * N], U8, name="w0", align_bytes=256)
-        w1 = keep.tile([P, 1, 2 * N], U8, name="w1", align_bytes=256)
-        w23 = keep.tile([P, 2, 2 * N], U8, name="w23", align_bytes=256)
+        groups = ((0, 1), (1, 2), (2, A))
+        xw, ww = [], []
+        for a0, a1 in groups:
+            x_g = keep.tile([P, a1 - a0, 2 * T], U8, name="xw%d" % a0, align_bytes=256)
+            w_g = keep.tile([P, a1 - a0, 2 * N], U8, name="ww%d" % a0, align_bytes=256)
+            xw.append(x_g)
+            ww.append(w_g)
         xs = keep.tile([P, A, T], U8, name="xs", align_bytes=256)
         ws0 = keep.tile([P, 1, N], U8, name="ws0", align_bytes=256)
         ws123 = keep.tile([P, A - 1, N], U8, name="ws123", align_bytes=256)
@@ -44,13 +45,17 @@ def tile_mix_xres_tm_mul_kernel(tc, x4_words, x4_scales, xr, w4_words, w4_scales
         for plane in (ws0, xs, ws123):
             nc.vector.memset(flat_i32(plane), 0)
 
-        def load_scales(queue, tile, dram, a0, a1):
+        def load_scales(tile, dram, a0, a1):
             n4 = dram.shape[2] // 4
             for r in range(4):
-                queue.dma_start(
+                nc.sync.dma_start(
                     out=flat_i32(tile)[r:P:32, :].rearrange("q (a n) -> q a n", n=n4),
                     in_=dram.bitcast(I32)[a0:a1, r:16:4, :].rearrange("a q n -> q a n"),
                 )
+
+        def load_words(tiles, dram, i):
+            a0, a1 = groups[i]
+            nc.sync.dma_start(out=tiles[i][:], in_=dram[a0:a1].rearrange("a p n -> p a n"))
 
         raw = []
         for a, widths in enumerate(((P, T - P), (T,), (T,), (T,))):
@@ -68,42 +73,45 @@ def tile_mix_xres_tm_mul_kernel(tc, x4_words, x4_scales, xr, w4_words, w4_scales
             )
 
         load_raw(0, 0)
-        load_scales(nc.sync, ws0, w4_scales, 0, 1)
-        nc.sync.dma_start(out=w0[:, 0, :], in_=w4_words[0])
-        nc.sync.dma_start(out=x0[:, 0, :], in_=x4_words[0])
-        load_scales(nc.sync, xs, x4_scales, 0, A)
+        load_scales(ws0, w4_scales, 0, 1)
+        load_words(ww, w4_words, 0)
+        load_words(xw, x4_words, 0)
+        load_scales(xs, x4_scales, 0, A)
         load_raw(0, 1)
-        load_scales(nc.gpsimd, ws123, w4_scales, 1, A)
-        nc.sync.dma_start(out=w1[:, 0, :], in_=w4_words[1])
-        nc.sync.dma_start(out=x123[:], in_=x4_words[1:A].rearrange("a p n -> p a n"))
-        nc.sync.dma_start(out=w23[:], in_=w4_words[2:A].rearrange("a p n -> p a n"))
+        load_words(ww, w4_words, 1)
+        load_words(xw, x4_words, 1)
+        load_scales(ws123, w4_scales, 1, A)
+        load_words(xw, x4_words, 2)
+        load_words(ww, w4_words, 2)
         for a in range(1, A):
             load_raw(a, 0)
         g_sb = []
-        for u in range(TT // 2):
-            g_u = keep.tile([P, 2, N], F32, name="g%d" % u, align_bytes=256)
-            nc.sync.dma_start(out=g_u[:], in_=g[2 * P * u : 2 * P * (u + 1), :].rearrange("(b p) n -> p b n", p=P))
-            g_sb.append(g_u)
+        for t in range(TT):
+            g_t = keep.tile([P, N], F32, name="g%d" % t, align_bytes=256)
+            nc.sync.dma_start(out=g_t[:], in_=g[P * t : P * (t + 1), :])
+            g_sb.append(g_t)
 
         banks = []
         for i in range(TT * NH):
             bank = psum.tile([P, HALF], F32, name="bank%d" % i)
             banks.append(bank)
 
+        def words_of(tiles, a):
+            i = min(a, len(groups) - 1)
+            return tiles[i][:, a - groups[i][0], :]
+
         def w_operand(a, h):
-            words, b = ((w0, 0), (w1, 0), (w23, 0), (w23, 1))[a]
             plane, c = (ws0, 0) if a == 0 else (ws123, a - 1)
             return (
-                words[:, b, 2 * HALF * h : 2 * HALF * (h + 1)].bitcast(FP4X4),
+                words_of(ww, a)[:, 2 * HALF * h : 2 * HALF * (h + 1)].bitcast(FP4X4),
                 plane[:, c, HALF * h : HALF * (h + 1)],
             )
 
         def x4_pass(a, t, h):
-            words, b = (x0, 0) if a == 0 else (x123, a - 1)
             rhs, rhs_scale = w_operand(a, h)
             nc.tensor.matmul_mx(
                 out=banks[NH * t + h][:],
-                lhsT=words[:, b, 2 * P * t : 2 * P * (t + 1)].bitcast(FP4X4),
+                lhsT=words_of(xw, a)[:, 2 * P * t : 2 * P * (t + 1)].bitcast(FP4X4),
                 lhsT_scale=xs[:, a, P * t : P * (t + 1)],
                 rhs=rhs,
                 rhs_scale=rhs_scale,
@@ -149,27 +157,33 @@ def tile_mix_xres_tm_mul_kernel(tc, x4_words, x4_scales, xr, w4_words, w4_scales
 
         interleave(nc.vector.tensor_copy, 0, 0, P)
         quantize(0, 0, P)
-        for a in range(A):
+        for a in range(A - 1):
             v0 = P if a == 0 else 0
             interleave(nc.vector.tensor_copy, a, v0, VCOLS)
             interleave(nc.scalar.copy, a, VCOLS, T)
             quantize(a, v0, VCOLS)
             quantize(a, VCOLS, T)
+        last = A - 1
+        interleave(nc.vector.tensor_copy, last, 0, P)
+        interleave(nc.scalar.copy, last, P, 2 * P)
+        interleave(nc.scalar.copy, last, 2 * P, 3 * P)
+        quantize(last, 0, P)
+        interleave(nc.vector.tensor_copy, last, 3 * P, T)
+        quantize(last, P, 2 * P)
+        quantize(last, 2 * P, T)
 
         for h in range(NH):
             xr_pass(0, 0, h)
-        for h in range(NH):
-            for t in range(TT):
-                x4_pass(0, t, h)
-        for t in range(1, TT):
-            for h in range(NH):
-                xr_pass(0, t, h)
-        for a in range(1, A):
+        for a in range(A):
             for h in range(NH):
                 for t in range(TT):
                     x4_pass(a, t, h)
+            if a == 0:
+                for t in range(1, TT):
+                    for h in range(NH):
+                        xr_pass(0, t, h)
         for a in range(1, A - 1):
-            for t in range(EARLY):
+            for t in range(last - a):
                 for h in range(NH):
                     xr_pass(a, t, h)
 
@@ -177,7 +191,7 @@ def tile_mix_xres_tm_mul_kernel(tc, x4_words, x4_scales, xr, w4_words, w4_scales
             result = keep.tile([P, N], F32, name="result%d" % t, align_bytes=256)
             rows = slice(P * t, P * (t + 1))
             for h in range(NH):
-                for a in range(A - 1 if t < EARLY else 1, A):
+                for a in range(max(last - t, 1), A):
                     xr_pass(a, t, h)
                 parts = 2 if (t, h) == (TT - 1, NH - 1) else 1
                 for j in range(parts):
@@ -186,7 +200,7 @@ def tile_mix_xres_tm_mul_kernel(tc, x4_words, x4_scales, xr, w4_words, w4_scales
                     nc.vector.tensor_tensor(
                         out=result[:, cols],
                         in0=banks[NH * t + h][:, b_cols],
-                        in1=g_sb[t // 2][:, t % 2, cols],
+                        in1=g_sb[t][:, cols],
                         op=mybir.AluOpType.mult,
                     )
                     if t == TT - 1:

@@ -18,6 +18,7 @@ A = K // 512
 TT = T // P
 NH = 2
 HALF = N // NH
+NARROW = 256
 VCOLS = 256
 
 
@@ -96,28 +97,33 @@ def tile_mix_xres_tm_mul_kernel(tc, x4_words, x4_scales, xr, w4_words, w4_scales
             bank = psum.tile([P, HALF], F32, name="bank%d" % i)
             banks.append(bank)
 
+        last_t = TT - 1
+        last_a = A - 1
+        sums = [(t, HALF * h, HALF, banks[NH * t + h][:]) for t in range(TT) for h in range(NH)]
+        sums[-1] = (last_t, HALF, NARROW, banks[-1][:, :NARROW])
+        closing = (last_t, N - NARROW, NARROW, banks[0][:, :NARROW])
+
         def words_of(tiles, a):
             i = min(a, len(groups) - 1)
             return tiles[i][:, a - groups[i][0], :]
 
-        def w_operand(a, h):
+        def mx_pass(lhs, lhs_scale, a, one, start, stop):
+            n0, width, acc = one[1:]
             plane, c = (ws0, 0) if a == 0 else (ws123, a - 1)
-            return (
-                words_of(ww, a)[:, 2 * HALF * h : 2 * HALF * (h + 1)].bitcast(FP4X4),
-                plane[:, c, HALF * h : HALF * (h + 1)],
+            nc.tensor.matmul_mx(
+                out=acc,
+                lhsT=lhs,
+                lhsT_scale=lhs_scale,
+                rhs=words_of(ww, a)[:, 2 * n0 : 2 * (n0 + width)].bitcast(FP4X4),
+                rhs_scale=plane[:, c, n0 : n0 + width],
+                start=start,
+                stop=stop,
             )
 
-        def x4_pass(a, t, h):
-            rhs, rhs_scale = w_operand(a, h)
-            nc.tensor.matmul_mx(
-                out=banks[NH * t + h][:],
-                lhsT=words_of(xw, a)[:, 2 * P * t : 2 * P * (t + 1)].bitcast(FP4X4),
-                lhsT_scale=xs[:, a, P * t : P * (t + 1)],
-                rhs=rhs,
-                rhs_scale=rhs_scale,
-                start=(a == 0 and t > 0),
-                stop=False,
-            )
+        def x4_pass(a, one, start=False):
+            t = one[0]
+            lhs = words_of(xw, a)[:, 2 * P * t : 2 * P * (t + 1)].bitcast(FP4X4)
+            mx_pass(lhs, xs[:, a, P * t : P * (t + 1)], a, one, start, False)
 
         xb, codes, scales = [], [], []
         for a in range(A):
@@ -143,67 +149,72 @@ def tile_mix_xres_tm_mul_kernel(tc, x4_words, x4_scales, xr, w4_words, w4_scales
                 in_=xb[a][:, t0:t1, :].rearrange("p t j -> p (t j)"),
             )
 
-        def xr_pass(a, t, h):
-            rhs, rhs_scale = w_operand(a, h)
-            nc.tensor.matmul_mx(
-                out=banks[NH * t + h][:],
-                lhsT=codes[a][:, P * t : P * (t + 1)].bitcast(FP8X4),
-                lhsT_scale=scales[a][:, P * t : P * (t + 1)],
-                rhs=rhs,
-                rhs_scale=rhs_scale,
-                start=(a == 0 and t == 0),
-                stop=(a == A - 1),
-            )
+        def xr_pass(a, one, start=False):
+            t = one[0]
+            lhs = codes[a][:, P * t : P * (t + 1)].bitcast(FP8X4)
+            mx_pass(lhs, scales[a][:, P * t : P * (t + 1)], a, one, start, a == last_a)
 
         interleave(nc.vector.tensor_copy, 0, 0, P)
         quantize(0, 0, P)
-        for a in range(A - 1):
+        for a in range(last_a):
             v0 = P if a == 0 else 0
             interleave(nc.vector.tensor_copy, a, v0, VCOLS)
             interleave(nc.scalar.copy, a, VCOLS, T)
             quantize(a, v0, VCOLS)
             quantize(a, VCOLS, T)
-        last = A - 1
-        interleave(nc.vector.tensor_copy, last, 0, P)
-        interleave(nc.scalar.copy, last, P, 2 * P)
-        interleave(nc.scalar.copy, last, 2 * P, 3 * P)
-        quantize(last, 0, P)
-        interleave(nc.vector.tensor_copy, last, 3 * P, T)
-        quantize(last, P, 2 * P)
-        quantize(last, 2 * P, T)
+        interleave(nc.vector.tensor_copy, last_a, 0, P)
+        for t in range(1, TT):
+            interleave(nc.scalar.copy, last_a, P * t, P * (t + 1))
+        quantize(last_a, 0, P)
+        quantize(last_a, P, 2 * P)
 
-        for h in range(NH):
-            xr_pass(0, 0, h)
-        for a in range(A):
-            for h in range(NH):
-                for t in range(TT):
-                    x4_pass(a, t, h)
-            if a == 0:
-                for t in range(1, TT):
-                    for h in range(NH):
-                        xr_pass(0, t, h)
-        for a in range(1, A - 1):
-            for t in range(last - a):
-                for h in range(NH):
-                    xr_pass(a, t, h)
+        for one in sums[:NH]:
+            xr_pass(0, one, start=True)
+        for one in sums:
+            x4_pass(0, one, start=one[0] > 0)
+        for one in sums[NH:]:
+            xr_pass(0, one)
+        for a in range(1, A):
+            for one in sums:
+                if (a, one[0]) != (last_a, last_t):
+                    x4_pass(a, one)
+        for one in sums[: NH * last_t]:
+            xr_pass(1, one)
+        for one in sums[:NH]:
+            xr_pass(2, one)
 
+        results = []
         for t in range(TT):
             result = keep.tile([P, N], F32, name="result%d" % t, align_bytes=256)
-            rows = slice(P * t, P * (t + 1))
-            for h in range(NH):
-                for a in range(max(last - t, 1), A):
-                    xr_pass(a, t, h)
-                parts = 2 if (t, h) == (TT - 1, NH - 1) else 1
-                for j in range(parts):
-                    b_cols = slice(HALF // parts * j, HALF // parts * (j + 1))
-                    cols = slice(HALF * h + b_cols.start, HALF * h + b_cols.stop)
-                    nc.vector.tensor_tensor(
-                        out=result[:, cols],
-                        in0=banks[NH * t + h][:, b_cols],
-                        in1=g_sb[t][:, cols],
-                        op=mybir.AluOpType.mult,
-                    )
-                    if t == TT - 1:
-                        nc.sync.dma_start(out=out[rows, cols], in_=result[:, cols])
-            if t < TT - 1:
-                nc.sync.dma_start(out=out[rows, :], in_=result[:])
+            results.append(result)
+
+        def times_g(one):
+            t, n0, width, acc = one
+            nc.vector.tensor_tensor(
+                out=results[t][:, n0 : n0 + width],
+                in0=acc,
+                in1=g_sb[t][:, n0 : n0 + width],
+                op=mybir.AluOpType.mult,
+            )
+
+        def store(t, n0, n1):
+            nc.sync.dma_start(out=out[P * t : P * (t + 1), n0:n1], in_=results[t][:, n0:n1])
+
+        first_left = (3, 2, 2, 1)
+        for i, one in enumerate(sums):
+            t = one[0]
+            if t == last_t:
+                x4_pass(last_a, one)
+            for a in range(first_left[t], A):
+                xr_pass(a, one)
+            times_g(one)
+            if i % NH == NH - 1:
+                store(t, 0, one[1] + one[2])
+                if t + 2 < TT:
+                    quantize(last_a, P * (t + 2), P * (t + 3))
+        for a in range(A):
+            x4_pass(a, closing, start=a == 0)
+        for a in range(A):
+            xr_pass(a, closing)
+        times_g(closing)
+        store(last_t, N - NARROW, N)

@@ -77,9 +77,9 @@ def tile_mix_xres_tm_mul_kernel(tc, x4_words, x4_scales, xr, w4_words, w4_scales
         load_scales(ws0, w4_scales, 0, 1)
         load_words(ww, w4_words, 0)
         load_words(xw, x4_words, 0)
+        load_words(ww, w4_words, 1)
         load_scales(xs, x4_scales, 0, A)
         load_raw(0, 1)
-        load_words(ww, w4_words, 1)
         load_words(xw, x4_words, 1)
         load_scales(ws123, w4_scales, 1, A)
         load_words(xw, x4_words, 2)

@@ -19,6 +19,7 @@ TT = T // P
 NH = 2
 HALF = N // NH
 NARROW = 256
+WARM = 5
 VCOLS = 256
 
 
@@ -29,22 +30,31 @@ def tile_mix_xres_tm_mul_kernel(tc, x4_words, x4_scales, xr, w4_words, w4_scales
         psum = ctx.enter_context(tc.psum_pool(name="psum", bufs=1))
         ctx.enter_context(tc.manual_schedule())
 
-        groups = ((0, 1), (1, 2), (2, A))
-        xw, ww = [], []
-        for a0, a1 in groups:
-            x_g = keep.tile([P, a1 - a0, 2 * T], U8, name="xw%d" % a0, align_bytes=256)
-            w_g = keep.tile([P, a1 - a0, 2 * N], U8, name="ww%d" % a0, align_bytes=256)
-            xw.append(x_g)
-            ww.append(w_g)
+        last_t = TT - 1
+        last_a = A - 1
+        xw_early = keep.tile([P, last_a, 2 * T], U8, name="xw_early", align_bytes=256)
+        xw_last = keep.tile([P, 1, 2 * T], U8, name="xw_last", align_bytes=256)
+        ww, raw = [], []
+        for a in range(A):
+            w_a = keep.tile([P, 2 * N], U8, name="ww%d" % a, align_bytes=256)
+            raw_a = keep.tile([P, 4, T], F32, name="raw%d" % a, align_bytes=256)
+            ww.append(w_a)
+            raw.append(raw_a)
         xs = keep.tile([P, A, T], U8, name="xs", align_bytes=256)
-        ws0 = keep.tile([P, 1, N], U8, name="ws0", align_bytes=256)
-        ws123 = keep.tile([P, A - 1, N], U8, name="ws123", align_bytes=256)
+        ws01 = keep.tile([P, 2, N], U8, name="ws01", align_bytes=256)
+        ws23 = keep.tile([P, 2, N], U8, name="ws23", align_bytes=256)
 
         def flat_i32(t):
             return t[:].rearrange("p a n -> p (a n)").bitcast(I32)
 
-        for plane in (ws0, xs, ws123):
-            nc.vector.memset(flat_i32(plane), 0)
+        zeros = keep.tile([P, 4 * HALF], BF16, name="zeros", align_bytes=256)
+        zero_codes = keep.tile([P, HALF], U32, name="zero_codes", align_bytes=256)
+        zero_scales = keep.tile([P, HALF], U8, name="zero_scales", align_bytes=256)
+        nc.vector.memset(flat_i32(ws01), 0)
+        nc.vector.memset(zeros[:].bitcast(I32), 0)
+        nc.vector.memset(flat_i32(xs), 0)
+        nc.vector.quantize_mx(out=zero_codes[:].bitcast(FP8X4), scales=zero_scales[:], in_=zeros[:])
+        nc.vector.memset(flat_i32(ws23), 0)
 
         def load_scales(tile, dram, a0, a1):
             n4 = dram.shape[2] // 4
@@ -54,38 +64,28 @@ def tile_mix_xres_tm_mul_kernel(tc, x4_words, x4_scales, xr, w4_words, w4_scales
                     in_=dram.bitcast(I32)[a0:a1, r:16:4, :].rearrange("a q n -> q a n"),
                 )
 
-        def load_words(tiles, dram, i):
-            a0, a1 = groups[i]
-            nc.sync.dma_start(out=tiles[i][:], in_=dram[a0:a1].rearrange("a p n -> p a n"))
+        def load_x(tile, a0, a1):
+            nc.sync.dma_start(out=tile[:], in_=x4_words[a0:a1].rearrange("a p n -> p a n"))
 
-        raw = []
-        for a, widths in enumerate(((P, T - P), (T,), (T,), (T,))):
-            pieces, t0 = [], 0
-            for width in widths:
-                piece = keep.tile([P, 4, width], F32, name="raw%d_%d" % (a, t0), align_bytes=256)
-                pieces.append((t0, t0 + width, piece))
-                t0 += width
-            raw.append(pieces)
+        def load_w(a):
+            nc.sync.dma_start(out=ww[a][:], in_=w4_words[a])
 
-        def load_raw(a, i):
-            t0, t1, piece = raw[a][i]
-            nc.sync.dma_start(
-                out=piece[:], in_=xr[512 * a : 512 * (a + 1), t0:t1].rearrange("(p j) t -> p j t", j=4)
-            )
+        def load_raw(a):
+            nc.sync.dma_start(out=raw[a][:], in_=xr[512 * a : 512 * (a + 1), :].rearrange("(p j) t -> p j t", j=4))
 
-        load_raw(0, 0)
-        load_scales(ws0, w4_scales, 0, 1)
-        load_words(ww, w4_words, 0)
-        load_words(xw, x4_words, 0)
-        load_words(ww, w4_words, 1)
+        load_raw(0)
+        load_w(0)
+        load_scales(ws01, w4_scales, 0, 2)
+        load_x(xw_early, 0, last_a)
+        load_w(1)
         load_scales(xs, x4_scales, 0, A)
-        load_raw(0, 1)
-        load_words(xw, x4_words, 1)
-        load_scales(ws123, w4_scales, 1, A)
-        load_words(xw, x4_words, 2)
-        load_words(ww, w4_words, 2)
-        for a in range(1, A):
-            load_raw(a, 0)
+        load_raw(1)
+        load_w(2)
+        load_scales(ws23, w4_scales, 2, A)
+        load_raw(2)
+        load_raw(last_a)
+        load_w(last_a)
+        load_x(xw_last, last_a, A)
         g_sb = []
         for t in range(TT):
             g_t = keep.tile([P, N], F32, name="g%d" % t, align_bytes=256)
@@ -97,32 +97,38 @@ def tile_mix_xres_tm_mul_kernel(tc, x4_words, x4_scales, xr, w4_words, w4_scales
             bank = psum.tile([P, HALF], F32, name="bank%d" % i)
             banks.append(bank)
 
-        last_t = TT - 1
-        last_a = A - 1
         sums = [(t, HALF * h, HALF, banks[NH * t + h][:]) for t in range(TT) for h in range(NH)]
         sums[-1] = (last_t, HALF, NARROW, banks[-1][:, :NARROW])
         closing = (last_t, N - NARROW, NARROW, banks[0][:, :NARROW])
 
-        def words_of(tiles, a):
-            i = min(a, len(groups) - 1)
-            return tiles[i][:, a - groups[i][0], :]
+        for i in range(WARM):
+            nc.tensor.matmul_mx(
+                out=banks[-1][:],
+                lhsT=zero_codes[:, : P // 2].bitcast(FP4X4),
+                lhsT_scale=zero_scales[:, :P],
+                rhs=zero_codes[:].bitcast(FP8X4),
+                rhs_scale=zero_scales[:],
+                start=True,
+                stop=True,
+            )
 
         def mx_pass(lhs, lhs_scale, a, one, start, stop):
             n0, width, acc = one[1:]
-            plane, c = (ws0, 0) if a == 0 else (ws123, a - 1)
+            plane = ws01 if a < 2 else ws23
             nc.tensor.matmul_mx(
                 out=acc,
                 lhsT=lhs,
                 lhsT_scale=lhs_scale,
-                rhs=words_of(ww, a)[:, 2 * n0 : 2 * (n0 + width)].bitcast(FP4X4),
-                rhs_scale=plane[:, c, n0 : n0 + width],
+                rhs=ww[a][:, 2 * n0 : 2 * (n0 + width)].bitcast(FP4X4),
+                rhs_scale=plane[:, a % 2, n0 : n0 + width],
                 start=start,
                 stop=stop,
             )
 
         def x4_pass(a, one, start=False):
             t = one[0]
-            lhs = words_of(xw, a)[:, 2 * P * t : 2 * P * (t + 1)].bitcast(FP4X4)
+            words = xw_early[:, a, :] if a < last_a else xw_last[:, 0, :]
+            lhs = words[:, 2 * P * t : 2 * P * (t + 1)].bitcast(FP4X4)
             mx_pass(lhs, xs[:, a, P * t : P * (t + 1)], a, one, start, False)
 
         xb, codes, scales = [], [], []
@@ -135,12 +141,10 @@ def tile_mix_xres_tm_mul_kernel(tc, x4_words, x4_scales, xr, w4_words, w4_scales
             scales.append(s_a)
 
         def interleave(copy, a, t0, t1):
-            for p0, p1, piece in raw[a]:
-                if p0 <= t0 and t1 <= p1:
-                    copy(
-                        xb[a][:, t0:t1, :].rearrange("p (c i) j -> p c j i", i=4),
-                        piece[:, :, t0 - p0 : t1 - p0].rearrange("p j (c i) -> p c j i", i=4),
-                    )
+            copy(
+                xb[a][:, t0:t1, :].rearrange("p (c i) j -> p c j i", i=4),
+                raw[a][:, :, t0:t1].rearrange("p j (c i) -> p c j i", i=4),
+            )
 
         def quantize(a, t0, t1):
             nc.vector.quantize_mx(
@@ -154,13 +158,10 @@ def tile_mix_xres_tm_mul_kernel(tc, x4_words, x4_scales, xr, w4_words, w4_scales
             lhs = codes[a][:, P * t : P * (t + 1)].bitcast(FP8X4)
             mx_pass(lhs, scales[a][:, P * t : P * (t + 1)], a, one, start, a == last_a)
 
-        interleave(nc.vector.tensor_copy, 0, 0, P)
-        quantize(0, 0, P)
         for a in range(last_a):
-            v0 = P if a == 0 else 0
-            interleave(nc.vector.tensor_copy, a, v0, VCOLS)
+            interleave(nc.vector.tensor_copy, a, 0, VCOLS)
             interleave(nc.scalar.copy, a, VCOLS, T)
-            quantize(a, v0, VCOLS)
+            quantize(a, 0, VCOLS)
             quantize(a, VCOLS, T)
         interleave(nc.vector.tensor_copy, last_a, 0, P)
         for t in range(1, TT):
@@ -168,20 +169,15 @@ def tile_mix_xres_tm_mul_kernel(tc, x4_words, x4_scales, xr, w4_words, w4_scales
         quantize(last_a, 0, P)
         quantize(last_a, P, 2 * P)
 
-        for one in sums[:NH]:
+        for one in sums:
             xr_pass(0, one, start=True)
         for one in sums:
-            x4_pass(0, one, start=one[0] > 0)
-        for one in sums[NH:]:
-            xr_pass(0, one)
-        for a in range(1, A):
+            x4_pass(0, one)
+        for a in range(1, last_a):
             for one in sums:
-                if (a, one[0]) != (last_a, last_t):
-                    x4_pass(a, one)
-        for one in sums[: NH * last_t]:
-            xr_pass(1, one)
-        for one in sums[:NH]:
-            xr_pass(2, one)
+                x4_pass(a, one)
+            for one in sums[: NH * last_t]:
+                xr_pass(a, one)
 
         results = []
         for t in range(TT):
@@ -200,12 +196,10 @@ def tile_mix_xres_tm_mul_kernel(tc, x4_words, x4_scales, xr, w4_words, w4_scales
         def store(t, n0, n1):
             nc.sync.dma_start(out=out[P * t : P * (t + 1), n0:n1], in_=results[t][:, n0:n1])
 
-        first_left = (3, 2, 2, 1)
         for i, one in enumerate(sums):
             t = one[0]
-            if t == last_t:
-                x4_pass(last_a, one)
-            for a in range(first_left[t], A):
+            x4_pass(last_a, one)
+            for a in range(1 if t == last_t else last_a, A):
                 xr_pass(a, one)
             times_g(one)
             if i % NH == NH - 1:

@@ -19,7 +19,7 @@ TT = T // P
 NH = 2
 HALF = N // NH
 NARROW = 256
-WARM = 5
+WARM = 6
 VCOLS = 256
 
 
@@ -32,8 +32,8 @@ def tile_mix_xres_tm_mul_kernel(tc, x4_words, x4_scales, xr, w4_words, w4_scales
 
         last_t = TT - 1
         last_a = A - 1
-        xw_early = keep.tile([P, last_a, 2 * T], U8, name="xw_early", align_bytes=256)
-        xw_last = keep.tile([P, 1, 2 * T], U8, name="xw_last", align_bytes=256)
+        xw_first = keep.tile([P, 1, 2 * T], U8, name="xw_first", align_bytes=256)
+        xw_rest = keep.tile([P, last_a, 2 * T], U8, name="xw_rest", align_bytes=256)
         ww, raw = [], []
         for a in range(A):
             w_a = keep.tile([P, 2 * N], U8, name="ww%d" % a, align_bytes=256)
@@ -41,8 +41,8 @@ def tile_mix_xres_tm_mul_kernel(tc, x4_words, x4_scales, xr, w4_words, w4_scales
             ww.append(w_a)
             raw.append(raw_a)
         xs = keep.tile([P, A, T], U8, name="xs", align_bytes=256)
-        ws01 = keep.tile([P, 2, N], U8, name="ws01", align_bytes=256)
-        ws23 = keep.tile([P, 2, N], U8, name="ws23", align_bytes=256)
+        ws_first = keep.tile([P, 1, N], U8, name="ws_first", align_bytes=256)
+        ws_rest = keep.tile([P, last_a, N], U8, name="ws_rest", align_bytes=256)
 
         def flat_i32(t):
             return t[:].rearrange("p a n -> p (a n)").bitcast(I32)
@@ -50,11 +50,11 @@ def tile_mix_xres_tm_mul_kernel(tc, x4_words, x4_scales, xr, w4_words, w4_scales
         zeros = keep.tile([P, 4 * HALF], BF16, name="zeros", align_bytes=256)
         zero_codes = keep.tile([P, HALF], U32, name="zero_codes", align_bytes=256)
         zero_scales = keep.tile([P, HALF], U8, name="zero_scales", align_bytes=256)
-        nc.vector.memset(flat_i32(ws01), 0)
         nc.vector.memset(zeros[:].bitcast(I32), 0)
-        nc.vector.memset(flat_i32(xs), 0)
+        nc.vector.memset(flat_i32(ws_first), 0)
         nc.vector.quantize_mx(out=zero_codes[:].bitcast(FP8X4), scales=zero_scales[:], in_=zeros[:])
-        nc.vector.memset(flat_i32(ws23), 0)
+        nc.vector.memset(flat_i32(xs), 0)
+        nc.vector.memset(flat_i32(ws_rest), 0)
 
         def load_scales(tile, dram, a0, a1):
             n4 = dram.shape[2] // 4
@@ -75,17 +75,16 @@ def tile_mix_xres_tm_mul_kernel(tc, x4_words, x4_scales, xr, w4_words, w4_scales
 
         load_raw(0)
         load_w(0)
-        load_scales(ws01, w4_scales, 0, 2)
-        load_x(xw_early, 0, last_a)
+        load_scales(ws_first, w4_scales, 0, 1)
+        load_x(xw_first, 0, 1)
         load_w(1)
         load_scales(xs, x4_scales, 0, A)
-        load_raw(1)
+        load_x(xw_rest, 1, A)
+        load_scales(ws_rest, w4_scales, 1, A)
         load_w(2)
-        load_scales(ws23, w4_scales, 2, A)
-        load_raw(2)
-        load_raw(last_a)
+        for a in range(1, A):
+            load_raw(a)
         load_w(last_a)
-        load_x(xw_last, last_a, A)
         g_sb = []
         for t in range(TT):
             g_t = keep.tile([P, N], F32, name="g%d" % t, align_bytes=256)
@@ -114,20 +113,20 @@ def tile_mix_xres_tm_mul_kernel(tc, x4_words, x4_scales, xr, w4_words, w4_scales
 
         def mx_pass(lhs, lhs_scale, a, one, start, stop):
             n0, width, acc = one[1:]
-            plane = ws01 if a < 2 else ws23
+            plane = ws_first[:, 0, :] if a == 0 else ws_rest[:, a - 1, :]
             nc.tensor.matmul_mx(
                 out=acc,
                 lhsT=lhs,
                 lhsT_scale=lhs_scale,
                 rhs=ww[a][:, 2 * n0 : 2 * (n0 + width)].bitcast(FP4X4),
-                rhs_scale=plane[:, a % 2, n0 : n0 + width],
+                rhs_scale=plane[:, n0 : n0 + width],
                 start=start,
                 stop=stop,
             )
 
         def x4_pass(a, one, start=False):
             t = one[0]
-            words = xw_early[:, a, :] if a < last_a else xw_last[:, 0, :]
+            words = xw_first[:, 0, :] if a == 0 else xw_rest[:, a - 1, :]
             lhs = words[:, 2 * P * t : 2 * P * (t + 1)].bitcast(FP4X4)
             mx_pass(lhs, xs[:, a, P * t : P * (t + 1)], a, one, start, False)
 
@@ -158,7 +157,19 @@ def tile_mix_xres_tm_mul_kernel(tc, x4_words, x4_scales, xr, w4_words, w4_scales
             lhs = codes[a][:, P * t : P * (t + 1)].bitcast(FP8X4)
             mx_pass(lhs, scales[a][:, P * t : P * (t + 1)], a, one, start, a == last_a)
 
-        for a in range(last_a):
+        hp = P // 2
+        interleave(nc.vector.tensor_copy, 0, 0, hp)
+        interleave(nc.scalar.copy, 0, hp, P)
+        interleave(nc.scalar.copy, 0, 2 * P, 3 * P)
+        interleave(nc.vector.tensor_copy, 0, P, P + hp)
+        quantize(0, 0, P)
+        interleave(nc.vector.tensor_copy, 0, P + hp, 2 * P)
+        interleave(nc.vector.tensor_copy, 0, 3 * P, 3 * P + hp)
+        quantize(0, P, 2 * P)
+        interleave(nc.vector.tensor_copy, 0, 3 * P + hp, T)
+        quantize(0, 2 * P, 3 * P)
+        quantize(0, 3 * P, T)
+        for a in range(1, last_a):
             interleave(nc.vector.tensor_copy, a, 0, VCOLS)
             interleave(nc.scalar.copy, a, VCOLS, T)
             quantize(a, 0, VCOLS)
@@ -171,13 +182,13 @@ def tile_mix_xres_tm_mul_kernel(tc, x4_words, x4_scales, xr, w4_words, w4_scales
 
         for one in sums:
             xr_pass(0, one, start=True)
-        for one in sums:
-            x4_pass(0, one)
-        for a in range(1, last_a):
+        for a in range(last_a):
             for one in sums:
                 x4_pass(a, one)
-            for one in sums[: NH * last_t]:
-                xr_pass(a, one)
+        for one in sums:
+            xr_pass(1, one)
+        for one in sums[: NH * last_t]:
+            xr_pass(2, one)
 
         results = []
         for t in range(TT):
@@ -199,7 +210,7 @@ def tile_mix_xres_tm_mul_kernel(tc, x4_words, x4_scales, xr, w4_words, w4_scales
         for i, one in enumerate(sums):
             t = one[0]
             x4_pass(last_a, one)
-            for a in range(1 if t == last_t else last_a, A):
+            for a in range(2 if t == last_t else last_a, A):
                 xr_pass(a, one)
             times_g(one)
             if i % NH == NH - 1:

@@ -32,8 +32,8 @@ def tile_mix_xres_tm_mul_kernel(tc, x4_words, x4_scales, xr, w4_words, w4_scales
 
         last_t = TT - 1
         last_a = A - 1
-        xw_first = keep.tile([P, 1, 2 * T], U8, name="xw_first", align_bytes=256)
-        xw_rest = keep.tile([P, last_a, 2 * T], U8, name="xw_rest", align_bytes=256)
+        xw_early = keep.tile([P, last_a, 2 * T], U8, name="xw_early", align_bytes=256)
+        xw_last = keep.tile([P, 1, 2 * T], U8, name="xw_last", align_bytes=256)
         ww, raw = [], []
         for a in range(A):
             w_a = keep.tile([P, 2 * N], U8, name="ww%d" % a, align_bytes=256)
@@ -41,20 +41,22 @@ def tile_mix_xres_tm_mul_kernel(tc, x4_words, x4_scales, xr, w4_words, w4_scales
             ww.append(w_a)
             raw.append(raw_a)
         xs = keep.tile([P, A, T], U8, name="xs", align_bytes=256)
-        ws_first = keep.tile([P, 1, N], U8, name="ws_first", align_bytes=256)
-        ws_rest = keep.tile([P, last_a, N], U8, name="ws_rest", align_bytes=256)
+        ws = keep.tile([P, A, N], U8, name="ws", align_bytes=256)
 
         def flat_i32(t):
             return t[:].rearrange("p a n -> p (a n)").bitcast(I32)
 
-        zeros = keep.tile([P, 4 * HALF], BF16, name="zeros", align_bytes=256)
         zero_codes = keep.tile([P, HALF], U32, name="zero_codes", align_bytes=256)
         zero_scales = keep.tile([P, HALF], U8, name="zero_scales", align_bytes=256)
-        nc.vector.memset(zeros[:].bitcast(I32), 0)
-        nc.vector.memset(flat_i32(ws_first), 0)
-        nc.vector.quantize_mx(out=zero_codes[:].bitcast(FP8X4), scales=zero_scales[:], in_=zeros[:])
+        nc.vector.memset(flat_i32(ws), 0)
         nc.vector.memset(flat_i32(xs), 0)
-        nc.vector.memset(flat_i32(ws_rest), 0)
+        zeros = xs[:].rearrange("p a n -> p (a n)").bitcast(BF16)
+        for c0 in range(0, HALF, HALF // 2):
+            nc.vector.quantize_mx(
+                out=zero_codes[:, c0 : c0 + HALF // 2].bitcast(FP8X4),
+                scales=zero_scales[:, c0 : c0 + HALF // 2],
+                in_=zeros,
+            )
 
         def load_scales(tile, dram, a0, a1):
             n4 = dram.shape[2] // 4
@@ -75,16 +77,16 @@ def tile_mix_xres_tm_mul_kernel(tc, x4_words, x4_scales, xr, w4_words, w4_scales
 
         load_raw(0)
         load_w(0)
-        load_scales(ws_first, w4_scales, 0, 1)
-        load_x(xw_first, 0, 1)
+        load_scales(ws, w4_scales, 0, A)
+        load_x(xw_early, 0, last_a)
         load_w(1)
         load_scales(xs, x4_scales, 0, A)
-        load_x(xw_rest, 1, A)
-        load_scales(ws_rest, w4_scales, 1, A)
+        load_raw(1)
         load_w(2)
-        for a in range(1, A):
-            load_raw(a)
+        load_raw(2)
+        load_raw(last_a)
         load_w(last_a)
+        load_x(xw_last, last_a, A)
         g_sb = []
         for t in range(TT):
             g_t = keep.tile([P, N], F32, name="g%d" % t, align_bytes=256)
@@ -113,20 +115,19 @@ def tile_mix_xres_tm_mul_kernel(tc, x4_words, x4_scales, xr, w4_words, w4_scales
 
         def mx_pass(lhs, lhs_scale, a, one, start, stop):
             n0, width, acc = one[1:]
-            plane = ws_first[:, 0, :] if a == 0 else ws_rest[:, a - 1, :]
             nc.tensor.matmul_mx(
                 out=acc,
                 lhsT=lhs,
                 lhsT_scale=lhs_scale,
                 rhs=ww[a][:, 2 * n0 : 2 * (n0 + width)].bitcast(FP4X4),
-                rhs_scale=plane[:, n0 : n0 + width],
+                rhs_scale=ws[:, a, n0 : n0 + width],
                 start=start,
                 stop=stop,
             )
 
         def x4_pass(a, one, start=False):
             t = one[0]
-            words = xw_first[:, 0, :] if a == 0 else xw_rest[:, a - 1, :]
+            words = xw_early[:, a, :] if a < last_a else xw_last[:, 0, :]
             lhs = words[:, 2 * P * t : 2 * P * (t + 1)].bitcast(FP4X4)
             mx_pass(lhs, xs[:, a, P * t : P * (t + 1)], a, one, start, False)
 
@@ -182,13 +183,13 @@ def tile_mix_xres_tm_mul_kernel(tc, x4_words, x4_scales, xr, w4_words, w4_scales
 
         for one in sums:
             xr_pass(0, one, start=True)
-        for a in range(last_a):
+        for one in sums:
+            x4_pass(0, one)
+        for a in range(1, last_a):
             for one in sums:
                 x4_pass(a, one)
-        for one in sums:
-            xr_pass(1, one)
-        for one in sums[: NH * last_t]:
-            xr_pass(2, one)
+            for one in sums[: NH * last_t]:
+                xr_pass(a, one)
 
         results = []
         for t in range(TT):
@@ -210,7 +211,7 @@ def tile_mix_xres_tm_mul_kernel(tc, x4_words, x4_scales, xr, w4_words, w4_scales
         for i, one in enumerate(sums):
             t = one[0]
             x4_pass(last_a, one)
-            for a in range(2 if t == last_t else last_a, A):
+            for a in range(1 if t == last_t else last_a, A):
                 xr_pass(a, one)
             times_g(one)
             if i % NH == NH - 1:

@@ -41,14 +41,15 @@ def tile_mix_xres_tm_mul_kernel(tc, x4_words, x4_scales, xr, w4_words, w4_scales
             ww.append(w_a)
             raw.append(raw_a)
         xs = keep.tile([P, A, T], U8, name="xs", align_bytes=256)
-        ws = keep.tile([P, A, N], U8, name="ws", align_bytes=256)
+        ws01 = keep.tile([P, 2, N], U8, name="ws01", align_bytes=256)
+        ws23 = keep.tile([P, 2, N], U8, name="ws23", align_bytes=256)
 
         def flat_i32(t):
             return t[:].rearrange("p a n -> p (a n)").bitcast(I32)
 
         zero_codes = keep.tile([P, HALF], U32, name="zero_codes", align_bytes=256)
         zero_scales = keep.tile([P, HALF], U8, name="zero_scales", align_bytes=256)
-        nc.vector.memset(flat_i32(ws), 0)
+        nc.vector.memset(flat_i32(ws01), 0)
         nc.vector.memset(flat_i32(xs), 0)
         zeros = xs[:].rearrange("p a n -> p (a n)").bitcast(BF16)
         for c0 in range(0, HALF, HALF // 2):
@@ -57,6 +58,7 @@ def tile_mix_xres_tm_mul_kernel(tc, x4_words, x4_scales, xr, w4_words, w4_scales
                 scales=zero_scales[:, c0 : c0 + HALF // 2],
                 in_=zeros,
             )
+        nc.vector.memset(flat_i32(ws23), 0)
 
         def load_scales(tile, dram, a0, a1):
             n4 = dram.shape[2] // 4
@@ -76,12 +78,13 @@ def tile_mix_xres_tm_mul_kernel(tc, x4_words, x4_scales, xr, w4_words, w4_scales
             nc.sync.dma_start(out=raw[a][:], in_=xr[512 * a : 512 * (a + 1), :].rearrange("(p j) t -> p j t", j=4))
 
         load_raw(0)
+        load_scales(ws01, w4_scales, 0, 2)
         load_w(0)
-        load_scales(ws, w4_scales, 0, A)
         load_x(xw_early, 0, last_a)
-        load_w(1)
         load_scales(xs, x4_scales, 0, A)
+        load_w(1)
         load_raw(1)
+        load_scales(ws23, w4_scales, 2, A)
         load_w(2)
         load_raw(2)
         load_raw(last_a)
@@ -115,12 +118,13 @@ def tile_mix_xres_tm_mul_kernel(tc, x4_words, x4_scales, xr, w4_words, w4_scales
 
         def mx_pass(lhs, lhs_scale, a, one, start, stop):
             n0, width, acc = one[1:]
+            plane = ws01 if a < 2 else ws23
             nc.tensor.matmul_mx(
                 out=acc,
                 lhsT=lhs,
                 lhsT_scale=lhs_scale,
                 rhs=ww[a][:, 2 * n0 : 2 * (n0 + width)].bitcast(FP4X4),
-                rhs_scale=ws[:, a, n0 : n0 + width],
+                rhs_scale=plane[:, a % 2, n0 : n0 + width],
                 start=start,
                 stop=stop,
             )
@@ -158,28 +162,27 @@ def tile_mix_xres_tm_mul_kernel(tc, x4_words, x4_scales, xr, w4_words, w4_scales
             lhs = codes[a][:, P * t : P * (t + 1)].bitcast(FP8X4)
             mx_pass(lhs, scales[a][:, P * t : P * (t + 1)], a, one, start, a == last_a)
 
-        hp = P // 2
-        interleave(nc.vector.tensor_copy, 0, 0, hp)
-        interleave(nc.scalar.copy, 0, hp, P)
-        interleave(nc.scalar.copy, 0, 2 * P, 3 * P)
-        interleave(nc.vector.tensor_copy, 0, P, P + hp)
-        quantize(0, 0, P)
-        interleave(nc.vector.tensor_copy, 0, P + hp, 2 * P)
-        interleave(nc.vector.tensor_copy, 0, 3 * P, 3 * P + hp)
-        quantize(0, P, 2 * P)
-        interleave(nc.vector.tensor_copy, 0, 3 * P + hp, T)
-        quantize(0, 2 * P, 3 * P)
-        quantize(0, 3 * P, T)
+        def tile_by_tile(a):
+            hp = P // 2
+            interleave(nc.vector.tensor_copy, a, 0, hp)
+            interleave(nc.scalar.copy, a, hp, P)
+            interleave(nc.scalar.copy, a, 2 * P, 3 * P)
+            interleave(nc.vector.tensor_copy, a, P, P + hp)
+            quantize(a, 0, P)
+            interleave(nc.vector.tensor_copy, a, P + hp, 2 * P)
+            interleave(nc.vector.tensor_copy, a, 3 * P, 3 * P + hp)
+            quantize(a, P, 2 * P)
+            interleave(nc.vector.tensor_copy, a, 3 * P + hp, T)
+            quantize(a, 2 * P, 3 * P)
+            quantize(a, 3 * P, T)
+
+        tile_by_tile(0)
         for a in range(1, last_a):
             interleave(nc.vector.tensor_copy, a, 0, VCOLS)
             interleave(nc.scalar.copy, a, VCOLS, T)
             quantize(a, 0, VCOLS)
             quantize(a, VCOLS, T)
-        interleave(nc.vector.tensor_copy, last_a, 0, P)
-        for t in range(1, TT):
-            interleave(nc.scalar.copy, last_a, P * t, P * (t + 1))
-        quantize(last_a, 0, P)
-        quantize(last_a, P, 2 * P)
+        tile_by_tile(last_a)
 
         for one in sums:
             xr_pass(0, one, start=True)
@@ -216,8 +219,6 @@ def tile_mix_xres_tm_mul_kernel(tc, x4_words, x4_scales, xr, w4_words, w4_scales
             times_g(one)
             if i % NH == NH - 1:
                 store(t, 0, one[1] + one[2])
-                if t + 2 < TT:
-                    quantize(last_a, P * (t + 2), P * (t + 3))
         for a in range(A):
             x4_pass(a, closing, start=a == 0)
         for a in range(A):

@@ -19,7 +19,7 @@ TT = T // P
 NH = 2
 HALF = N // NH
 NARROW = 256
-WARM = 6
+WARM_EARLY, WARM_LATE = 4, 2
 VCOLS = 256
 
 
@@ -32,8 +32,7 @@ def tile_mix_xres_tm_mul_kernel(tc, x4_words, x4_scales, xr, w4_words, w4_scales
 
         last_t = TT - 1
         last_a = A - 1
-        xw_early = keep.tile([P, last_a, 2 * T], U8, name="xw_early", align_bytes=256)
-        xw_last = keep.tile([P, 1, 2 * T], U8, name="xw_last", align_bytes=256)
+        xw = keep.tile([P, A, 2 * T], U8, name="xw", align_bytes=256)
         ww, raw = [], []
         for a in range(A):
             w_a = keep.tile([P, 2 * N], U8, name="ww%d" % a, align_bytes=256)
@@ -68,9 +67,6 @@ def tile_mix_xres_tm_mul_kernel(tc, x4_words, x4_scales, xr, w4_words, w4_scales
                     in_=dram.bitcast(I32)[a0:a1, r:16:4, :].rearrange("a q n -> q a n"),
                 )
 
-        def load_x(tile, a0, a1):
-            nc.sync.dma_start(out=tile[:], in_=x4_words[a0:a1].rearrange("a p n -> p a n"))
-
         def load_w(a):
             nc.sync.dma_start(out=ww[a][:], in_=w4_words[a])
 
@@ -80,7 +76,7 @@ def tile_mix_xres_tm_mul_kernel(tc, x4_words, x4_scales, xr, w4_words, w4_scales
         load_raw(0)
         load_scales(ws01, w4_scales, 0, 2)
         load_w(0)
-        load_x(xw_early, 0, last_a)
+        nc.sync.dma_start(out=xw[:], in_=x4_words.rearrange("a p n -> p a n"))
         load_scales(xs, x4_scales, 0, A)
         load_w(1)
         load_raw(1)
@@ -89,7 +85,6 @@ def tile_mix_xres_tm_mul_kernel(tc, x4_words, x4_scales, xr, w4_words, w4_scales
         load_raw(2)
         load_raw(last_a)
         load_w(last_a)
-        load_x(xw_last, last_a, A)
         g_sb = []
         for t in range(TT):
             g_t = keep.tile([P, N], F32, name="g%d" % t, align_bytes=256)
@@ -105,16 +100,19 @@ def tile_mix_xres_tm_mul_kernel(tc, x4_words, x4_scales, xr, w4_words, w4_scales
         sums[-1] = (last_t, HALF, NARROW, banks[-1][:, :NARROW])
         closing = (last_t, N - NARROW, NARROW, banks[0][:, :NARROW])
 
-        for i in range(WARM):
-            nc.tensor.matmul_mx(
-                out=banks[-1][:],
-                lhsT=zero_codes[:, : P // 2].bitcast(FP4X4),
-                lhsT_scale=zero_scales[:, :P],
-                rhs=zero_codes[:].bitcast(FP8X4),
-                rhs_scale=zero_scales[:],
-                start=True,
-                stop=True,
-            )
+        def warm_up(n, lhs):
+            for i in range(n):
+                nc.tensor.matmul_mx(
+                    out=banks[-1][:],
+                    lhsT=lhs.bitcast(FP4X4),
+                    lhsT_scale=zero_scales[:, :P],
+                    rhs=zero_codes[:].bitcast(FP8X4),
+                    rhs_scale=zero_scales[:],
+                    start=True,
+                    stop=True,
+                )
+
+        warm_up(WARM_EARLY, zero_codes[:, : P // 2])
 
         def mx_pass(lhs, lhs_scale, a, one, start, stop):
             n0, width, acc = one[1:]
@@ -131,8 +129,7 @@ def tile_mix_xres_tm_mul_kernel(tc, x4_words, x4_scales, xr, w4_words, w4_scales
 
         def x4_pass(a, one, start=False):
             t = one[0]
-            words = xw_early[:, a, :] if a < last_a else xw_last[:, 0, :]
-            lhs = words[:, 2 * P * t : 2 * P * (t + 1)].bitcast(FP4X4)
+            lhs = xw[:, a, 2 * P * t : 2 * P * (t + 1)].bitcast(FP4X4)
             mx_pass(lhs, xs[:, a, P * t : P * (t + 1)], a, one, start, False)
 
         xb, codes, scales = [], [], []
@@ -165,6 +162,10 @@ def tile_mix_xres_tm_mul_kernel(tc, x4_words, x4_scales, xr, w4_words, w4_scales
         def tile_by_tile(a):
             hp = P // 2
             interleave(nc.vector.tensor_copy, a, 0, hp)
+            if a == 0:
+                late = keep.tile([P, hp], U32, name="late", align_bytes=256)
+                nc.vector.tensor_copy(late[:].bitcast(I32), zero_codes[:, :hp].bitcast(I32))
+                warm_up(WARM_LATE, late[:])
             interleave(nc.scalar.copy, a, hp, P)
             interleave(nc.scalar.copy, a, 2 * P, 3 * P)
             interleave(nc.vector.tensor_copy, a, P, P + hp)

@@ -32,69 +32,67 @@ def tile_mix_xres_tm_mul_kernel(tc, x4_words, x4_scales, xr, w4_words, w4_scales
 
         last_t = TT - 1
         last_a = A - 1
-        xw = keep.tile([P, A, 2 * T], U8, name="xw", align_bytes=256)
-        ww, raw = [], []
-        for a in range(A):
-            w_a = keep.tile([P, 2 * N], U8, name="ww%d" % a, align_bytes=256)
-            raw_a = keep.tile([P, 4, T], F32, name="raw%d" % a, align_bytes=256)
-            ww.append(w_a)
-            raw.append(raw_a)
-        xs = keep.tile([P, A, T], U8, name="xs", align_bytes=256)
-        ws01 = keep.tile([P, 2, N], U8, name="ws01", align_bytes=256)
-        ws23 = keep.tile([P, 2, N], U8, name="ws23", align_bytes=256)
 
-        def flat_i32(t):
-            return t[:].rearrange("p a n -> p (a n)").bitcast(I32)
+        def sbuf(name, shape, dtype):
+            return keep.tile(shape, dtype, name=name, align_bytes=256)
 
-        zero_codes = keep.tile([P, HALF], U32, name="zero_codes", align_bytes=256)
-        zero_scales = keep.tile([P, HALF], U8, name="zero_scales", align_bytes=256)
-        nc.vector.memset(flat_i32(ws01), 0)
-        nc.vector.memset(flat_i32(xs), 0)
-        zeros = xs[:].rearrange("p a n -> p (a n)").bitcast(BF16)
+        def flat(tile, dtype):
+            return tile[:].rearrange("p a n -> p (a n)").bitcast(dtype)
+
+        xw01 = sbuf("xw01", [P, 2, 2 * T], U8)
+        xw23 = sbuf("xw23", [P, 2, 2 * T], U8)
+        ww = [sbuf("ww%d" % a, [P, 1, 2 * N], U8) for a in range(A)]
+        split = P * last_t
+        raw_head = sbuf("raw_head", [P, 4, split], F32)
+        raw_tail = sbuf("raw_tail", [P, 4, T - split], F32)
+        raw = [None] + [sbuf("raw%d" % a, [P, 4, T], F32) for a in range(1, A)]
+        g_sb = [sbuf("g%d" % t, [P, N], F32) for t in range(TT)]
+        xs = sbuf("xs", [P, A, T], U8)
+        ws = sbuf("ws", [P, A, N], U8)
+        zero_codes = sbuf("zero_codes", [P, HALF], U32)
+        zero_scales = sbuf("zero_scales", [P, HALF], U8)
+
+        for plane in (xs, ws):
+            nc.vector.memset(flat(plane, I32), 0)
         for c0 in range(0, HALF, HALF // 2):
             nc.vector.quantize_mx(
                 out=zero_codes[:, c0 : c0 + HALF // 2].bitcast(FP8X4),
                 scales=zero_scales[:, c0 : c0 + HALF // 2],
-                in_=zeros,
+                in_=flat(xs, BF16),
             )
-        nc.vector.memset(flat_i32(ws23), 0)
 
-        def load_scales(tile, dram, a0, a1):
+        def load_scales(plane, dram, a0, a1):
             n4 = dram.shape[2] // 4
             for r in range(4):
                 nc.sync.dma_start(
-                    out=flat_i32(tile)[r:P:32, :].rearrange("q (a n) -> q a n", n=n4),
+                    out=flat(plane, I32)[r:P:32, :].rearrange("q (a n) -> q a n", n=n4),
                     in_=dram.bitcast(I32)[a0:a1, r:16:4, :].rearrange("a q n -> q a n"),
                 )
 
-        def load_w(a):
-            nc.sync.dma_start(out=ww[a][:], in_=w4_words[a])
+        def load_words(tile, dram, a0, a1):
+            nc.sync.dma_start(out=tile[:], in_=dram[a0:a1].rearrange("a p n -> p a n"))
 
-        def load_raw(a):
-            nc.sync.dma_start(out=raw[a][:], in_=xr[512 * a : 512 * (a + 1), :].rearrange("(p j) t -> p j t", j=4))
+        def load_xr(tile, a, t0, t1):
+            rows = xr[512 * a : 512 * (a + 1), t0:t1]
+            nc.sync.dma_start(out=tile[:], in_=rows.rearrange("(p j) t -> p j t", j=4))
 
-        load_raw(0)
-        load_scales(ws01, w4_scales, 0, 2)
-        load_w(0)
-        nc.sync.dma_start(out=xw[:], in_=x4_words.rearrange("a p n -> p a n"))
+        load_xr(raw_head, 0, 0, split)
+        load_scales(ws, w4_scales, 0, A)
+        load_words(ww[0], w4_words, 0, 1)
+        load_xr(raw_tail, 0, split, T)
+        load_words(xw01, x4_words, 0, 2)
         load_scales(xs, x4_scales, 0, A)
-        load_w(1)
-        load_raw(1)
-        load_scales(ws23, w4_scales, 2, A)
-        load_w(2)
-        load_raw(2)
-        load_raw(last_a)
-        load_w(last_a)
-        g_sb = []
+        load_words(ww[1], w4_words, 1, 2)
+        load_xr(raw[1], 1, 0, T)
+        load_words(xw23, x4_words, 2, A)
+        load_words(ww[2], w4_words, 2, 3)
+        load_xr(raw[2], 2, 0, T)
+        load_xr(raw[last_a], last_a, 0, T)
+        load_words(ww[last_a], w4_words, last_a, A)
         for t in range(TT):
-            g_t = keep.tile([P, N], F32, name="g%d" % t, align_bytes=256)
-            nc.sync.dma_start(out=g_t[:], in_=g[P * t : P * (t + 1), :])
-            g_sb.append(g_t)
+            nc.sync.dma_start(out=g_sb[t][:], in_=g[P * t : P * (t + 1), :])
 
-        banks = []
-        for i in range(TT * NH):
-            bank = psum.tile([P, HALF], F32, name="bank%d" % i)
-            banks.append(bank)
+        banks = [psum.tile([P, HALF], F32, name="bank%d" % i) for i in range(TT * NH)]
 
         sums = [(t, HALF * h, HALF, banks[NH * t + h][:]) for t in range(TT) for h in range(NH)]
         sums[-1] = (last_t, HALF, NARROW, banks[-1][:, :NARROW])
@@ -116,35 +114,41 @@ def tile_mix_xres_tm_mul_kernel(tc, x4_words, x4_scales, xr, w4_words, w4_scales
 
         def mx_pass(lhs, lhs_scale, a, one, start, stop):
             n0, width, acc = one[1:]
-            plane = ws01 if a < 2 else ws23
             nc.tensor.matmul_mx(
                 out=acc,
                 lhsT=lhs,
                 lhsT_scale=lhs_scale,
-                rhs=ww[a][:, 2 * n0 : 2 * (n0 + width)].bitcast(FP4X4),
-                rhs_scale=plane[:, a % 2, n0 : n0 + width],
+                rhs=ww[a][:, 0, 2 * n0 : 2 * (n0 + width)].bitcast(FP4X4),
+                rhs_scale=ws[:, a, n0 : n0 + width],
                 start=start,
                 stop=stop,
             )
 
         def x4_pass(a, one, start=False):
             t = one[0]
-            lhs = xw[:, a, 2 * P * t : 2 * P * (t + 1)].bitcast(FP4X4)
+            words = xw01 if a < 2 else xw23
+            lhs = words[:, a % 2, 2 * P * t : 2 * P * (t + 1)].bitcast(FP4X4)
             mx_pass(lhs, xs[:, a, P * t : P * (t + 1)], a, one, start, False)
 
-        xb, codes, scales = [], [], []
-        for a in range(A):
-            xb_a = keep.tile([P, T, 4], BF16, name="xb%d" % a, align_bytes=256)
-            c_a = keep.tile([P, T], U32, name="codes%d" % a, align_bytes=256)
-            s_a = keep.tile([P, T], U8, name="scales%d" % a, align_bytes=256)
-            xb.append(xb_a)
-            codes.append(c_a)
-            scales.append(s_a)
+        xb = [sbuf("xb%d" % a, [P, T, 4], BF16) for a in range(A)]
+        codes = [sbuf("codes%d" % a, [P, T], U32) for a in range(A)]
+        scales = [sbuf("scales%d" % a, [P, T], U8) for a in range(A)]
+
+        def xr_pass(a, one, start=False):
+            t = one[0]
+            lhs = codes[a][:, P * t : P * (t + 1)].bitcast(FP8X4)
+            mx_pass(lhs, scales[a][:, P * t : P * (t + 1)], a, one, start, a == last_a)
 
         def interleave(copy, a, t0, t1):
+            if a > 0:
+                source = raw[a][:, :, t0:t1]
+            elif t0 < split:
+                source = raw_head[:, :, t0:t1]
+            else:
+                source = raw_tail[:, :, t0 - split : t1 - split]
             copy(
                 xb[a][:, t0:t1, :].rearrange("p (c i) j -> p c j i", i=4),
-                raw[a][:, :, t0:t1].rearrange("p j (c i) -> p c j i", i=4),
+                source.rearrange("p j (c i) -> p c j i", i=4),
             )
 
         def quantize(a, t0, t1):
@@ -154,36 +158,37 @@ def tile_mix_xres_tm_mul_kernel(tc, x4_words, x4_scales, xr, w4_words, w4_scales
                 in_=xb[a][:, t0:t1, :].rearrange("p t j -> p (t j)"),
             )
 
-        def xr_pass(a, one, start=False):
-            t = one[0]
-            lhs = codes[a][:, P * t : P * (t + 1)].bitcast(FP8X4)
-            mx_pass(lhs, scales[a][:, P * t : P * (t + 1)], a, one, start, a == last_a)
-
-        def tile_by_tile(a):
-            hp = P // 2
-            interleave(nc.vector.tensor_copy, a, 0, hp)
-            if a == 0:
-                late = keep.tile([P, hp], U32, name="late", align_bytes=256)
-                nc.vector.tensor_copy(late[:].bitcast(I32), zero_codes[:, :hp].bitcast(I32))
-                warm_up(WARM_LATE, late[:])
-            interleave(nc.scalar.copy, a, hp, P)
-            interleave(nc.scalar.copy, a, 2 * P, 3 * P)
-            interleave(nc.vector.tensor_copy, a, P, P + hp)
-            quantize(a, 0, P)
-            interleave(nc.vector.tensor_copy, a, P + hp, 2 * P)
-            interleave(nc.vector.tensor_copy, a, 3 * P, 3 * P + hp)
-            quantize(a, P, 2 * P)
-            interleave(nc.vector.tensor_copy, a, 3 * P + hp, T)
-            quantize(a, 2 * P, 3 * P)
-            quantize(a, 3 * P, T)
-
-        tile_by_tile(0)
+        hp = P // 2
+        interleave(nc.vector.tensor_copy, 0, 0, P)
+        interleave(nc.scalar.copy, 0, 2 * P, 3 * P)
+        interleave(nc.vector.tensor_copy, 0, P, 2 * P)
+        late = sbuf("late", [P, hp], U32)
+        nc.vector.tensor_copy(late[:].bitcast(I32), zero_codes[:, :hp].bitcast(I32))
+        warm_up(WARM_LATE, late[:])
+        quantize(0, 0, P)
+        quantize(0, P, 2 * P)
+        quantize(0, 2 * P, 3 * P)
+        interleave(nc.vector.tensor_copy, 0, 3 * P, 3 * P + hp)
+        interleave(nc.scalar.copy, 0, 3 * P + hp, T)
+        quantize(0, 3 * P, T)
         for a in range(1, last_a):
-            interleave(nc.vector.tensor_copy, a, 0, VCOLS)
+            interleave(nc.vector.tensor_copy, a, 0, P)
             interleave(nc.scalar.copy, a, VCOLS, T)
-            quantize(a, 0, VCOLS)
+            interleave(nc.vector.tensor_copy, a, P, VCOLS)
+            quantize(a, 0, P)
+            quantize(a, P, VCOLS)
             quantize(a, VCOLS, T)
-        tile_by_tile(last_a)
+        interleave(nc.vector.tensor_copy, last_a, 0, hp)
+        interleave(nc.scalar.copy, last_a, hp, P)
+        interleave(nc.scalar.copy, last_a, 2 * P, 3 * P)
+        interleave(nc.vector.tensor_copy, last_a, P, P + hp)
+        quantize(last_a, 0, P)
+        interleave(nc.vector.tensor_copy, last_a, P + hp, 2 * P)
+        interleave(nc.vector.tensor_copy, last_a, 3 * P, 3 * P + hp)
+        quantize(last_a, P, 2 * P)
+        interleave(nc.vector.tensor_copy, last_a, 3 * P + hp, T)
+        quantize(last_a, 2 * P, 3 * P)
+        quantize(last_a, 3 * P, T)
 
         for one in sums:
             xr_pass(0, one, start=True)
@@ -195,10 +200,7 @@ def tile_mix_xres_tm_mul_kernel(tc, x4_words, x4_scales, xr, w4_words, w4_scales
             for one in sums[: NH * last_t]:
                 xr_pass(a, one)
 
-        results = []
-        for t in range(TT):
-            result = keep.tile([P, N], F32, name="result%d" % t, align_bytes=256)
-            results.append(result)
+        results = [sbuf("result%d" % t, [P, N], F32) for t in range(TT)]
 
         def times_g(one):
             t, n0, width, acc = one

@@ -39,20 +39,20 @@ def tile_mix_xres_tm_mul_kernel(tc, x4_words, x4_scales, xr, w4_words, w4_scales
         def flat(tile, dtype):
             return tile[:].rearrange("p a n -> p (a n)").bitcast(dtype)
 
-        xw01 = sbuf("xw01", [P, 2, 2 * T], U8)
-        xw23 = sbuf("xw23", [P, 2, 2 * T], U8)
+        xw = sbuf("xw", [P, A, 2 * T], U8)
         ww = [sbuf("ww%d" % a, [P, 1, 2 * N], U8) for a in range(A)]
-        split = P * last_t
+        split = T // 2
         raw_head = sbuf("raw_head", [P, 4, split], F32)
         raw_tail = sbuf("raw_tail", [P, 4, T - split], F32)
         raw = [None] + [sbuf("raw%d" % a, [P, 4, T], F32) for a in range(1, A)]
         g_sb = [sbuf("g%d" % t, [P, N], F32) for t in range(TT)]
         xs = sbuf("xs", [P, A, T], U8)
-        ws = sbuf("ws", [P, A, N], U8)
+        ws01 = sbuf("ws01", [P, 2, N], U8)
+        ws23 = sbuf("ws23", [P, 2, N], U8)
         zero_codes = sbuf("zero_codes", [P, HALF], U32)
         zero_scales = sbuf("zero_scales", [P, HALF], U8)
 
-        for plane in (xs, ws):
+        for plane in (ws01, xs):
             nc.vector.memset(flat(plane, I32), 0)
         for c0 in range(0, HALF, HALF // 2):
             nc.vector.quantize_mx(
@@ -60,6 +60,7 @@ def tile_mix_xres_tm_mul_kernel(tc, x4_words, x4_scales, xr, w4_words, w4_scales
                 scales=zero_scales[:, c0 : c0 + HALF // 2],
                 in_=flat(xs, BF16),
             )
+        nc.vector.memset(flat(ws23, I32), 0)
 
         def load_scales(plane, dram, a0, a1):
             n4 = dram.shape[2] // 4
@@ -77,14 +78,14 @@ def tile_mix_xres_tm_mul_kernel(tc, x4_words, x4_scales, xr, w4_words, w4_scales
             nc.sync.dma_start(out=tile[:], in_=rows.rearrange("(p j) t -> p j t", j=4))
 
         load_xr(raw_head, 0, 0, split)
-        load_scales(ws, w4_scales, 0, A)
+        load_scales(ws01, w4_scales, 0, 2)
         load_words(ww[0], w4_words, 0, 1)
         load_xr(raw_tail, 0, split, T)
-        load_words(xw01, x4_words, 0, 2)
+        load_words(xw, x4_words, 0, A)
         load_scales(xs, x4_scales, 0, A)
         load_words(ww[1], w4_words, 1, 2)
         load_xr(raw[1], 1, 0, T)
-        load_words(xw23, x4_words, 2, A)
+        load_scales(ws23, w4_scales, 2, A)
         load_words(ww[2], w4_words, 2, 3)
         load_xr(raw[2], 2, 0, T)
         load_xr(raw[last_a], last_a, 0, T)
@@ -114,20 +115,20 @@ def tile_mix_xres_tm_mul_kernel(tc, x4_words, x4_scales, xr, w4_words, w4_scales
 
         def mx_pass(lhs, lhs_scale, a, one, start, stop):
             n0, width, acc = one[1:]
+            plane = ws01 if a < 2 else ws23
             nc.tensor.matmul_mx(
                 out=acc,
                 lhsT=lhs,
                 lhsT_scale=lhs_scale,
                 rhs=ww[a][:, 0, 2 * n0 : 2 * (n0 + width)].bitcast(FP4X4),
-                rhs_scale=ws[:, a, n0 : n0 + width],
+                rhs_scale=plane[:, a % 2, n0 : n0 + width],
                 start=start,
                 stop=stop,
             )
 
         def x4_pass(a, one, start=False):
             t = one[0]
-            words = xw01 if a < 2 else xw23
-            lhs = words[:, a % 2, 2 * P * t : 2 * P * (t + 1)].bitcast(FP4X4)
+            lhs = xw[:, a, 2 * P * t : 2 * P * (t + 1)].bitcast(FP4X4)
             mx_pass(lhs, xs[:, a, P * t : P * (t + 1)], a, one, start, False)
 
         xb = [sbuf("xb%d" % a, [P, T, 4], BF16) for a in range(A)]
@@ -160,16 +161,18 @@ def tile_mix_xres_tm_mul_kernel(tc, x4_words, x4_scales, xr, w4_words, w4_scales
 
         hp = P // 2
         interleave(nc.vector.tensor_copy, 0, 0, P)
-        interleave(nc.scalar.copy, 0, 2 * P, 3 * P)
-        interleave(nc.vector.tensor_copy, 0, P, 2 * P)
+        interleave(nc.scalar.copy, 0, P + hp, 2 * P)
+        interleave(nc.vector.tensor_copy, 0, P, P + hp)
+        quantize(0, 0, P)
+        quantize(0, P, 2 * P)
         late = sbuf("late", [P, hp], U32)
         nc.vector.tensor_copy(late[:].bitcast(I32), zero_codes[:, :hp].bitcast(I32))
         warm_up(WARM_LATE, late[:])
-        quantize(0, 0, P)
-        quantize(0, P, 2 * P)
-        quantize(0, 2 * P, 3 * P)
-        interleave(nc.vector.tensor_copy, 0, 3 * P, 3 * P + hp)
+        interleave(nc.vector.tensor_copy, 0, 2 * P, 2 * P + hp)
+        interleave(nc.scalar.copy, 0, 2 * P + hp, 3 * P)
         interleave(nc.scalar.copy, 0, 3 * P + hp, T)
+        interleave(nc.vector.tensor_copy, 0, 3 * P, 3 * P + hp)
+        quantize(0, 2 * P, 3 * P)
         quantize(0, 3 * P, T)
         for a in range(1, last_a):
             interleave(nc.vector.tensor_copy, a, 0, P)

@@ -39,7 +39,8 @@ def tile_mix_xres_tm_mul_kernel(tc, x4_words, x4_scales, xr, w4_words, w4_scales
         def flat(tile, dtype):
             return tile[:].rearrange("p a n -> p (a n)").bitcast(dtype)
 
-        xw = sbuf("xw", [P, A, 2 * T], U8)
+        xw01 = sbuf("xw01", [P, 2, 2 * T], U8)
+        xw23 = sbuf("xw23", [P, 2, 2 * T], U8)
         ww = [sbuf("ww%d" % a, [P, 1, 2 * N], U8) for a in range(A)]
         split = T // 2
         raw_head = sbuf("raw_head", [P, 4, split], F32)
@@ -81,11 +82,12 @@ def tile_mix_xres_tm_mul_kernel(tc, x4_words, x4_scales, xr, w4_words, w4_scales
         load_scales(ws01, w4_scales, 0, 2)
         load_words(ww[0], w4_words, 0, 1)
         load_xr(raw_tail, 0, split, T)
-        load_words(xw, x4_words, 0, A)
+        load_words(xw01, x4_words, 0, 2)
         load_scales(xs, x4_scales, 0, A)
         load_words(ww[1], w4_words, 1, 2)
         load_xr(raw[1], 1, 0, T)
         load_scales(ws23, w4_scales, 2, A)
+        load_words(xw23, x4_words, 2, A)
         load_words(ww[2], w4_words, 2, 3)
         load_xr(raw[2], 2, 0, T)
         load_xr(raw[last_a], last_a, 0, T)
@@ -128,7 +130,8 @@ def tile_mix_xres_tm_mul_kernel(tc, x4_words, x4_scales, xr, w4_words, w4_scales
 
         def x4_pass(a, one, start=False):
             t = one[0]
-            lhs = xw[:, a, 2 * P * t : 2 * P * (t + 1)].bitcast(FP4X4)
+            words = xw01 if a < 2 else xw23
+            lhs = words[:, a % 2, 2 * P * t : 2 * P * (t + 1)].bitcast(FP4X4)
             mx_pass(lhs, xs[:, a, P * t : P * (t + 1)], a, one, start, False)
 
         xb = [sbuf("xb%d" % a, [P, T, 4], BF16) for a in range(A)]

@@ -19,7 +19,6 @@ TT = T // P
 NH = 2
 HALF = N // NH
 NARROW = 256
-WARM_EARLY, WARM_LATE = 4, 2
 VCOLS = 256
 
 
@@ -50,17 +49,9 @@ def tile_mix_xres_tm_mul_kernel(tc, x4_words, x4_scales, xr, w4_words, w4_scales
         xs = sbuf("xs", [P, A, T], U8)
         ws01 = sbuf("ws01", [P, 2, N], U8)
         ws23 = sbuf("ws23", [P, 2, N], U8)
-        zero_codes = sbuf("zero_codes", [P, HALF], U32)
-        zero_scales = sbuf("zero_scales", [P, HALF], U8)
 
         for plane in (ws01, xs):
             nc.vector.memset(flat(plane, I32), 0)
-        for c0 in range(0, HALF, HALF // 2):
-            nc.vector.quantize_mx(
-                out=zero_codes[:, c0 : c0 + HALF // 2].bitcast(FP8X4),
-                scales=zero_scales[:, c0 : c0 + HALF // 2],
-                in_=flat(xs, BF16),
-            )
         nc.vector.memset(flat(ws23, I32), 0)
 
         def load_scales(plane, dram, a0, a1):
@@ -100,20 +91,6 @@ def tile_mix_xres_tm_mul_kernel(tc, x4_words, x4_scales, xr, w4_words, w4_scales
         sums = [(t, HALF * h, HALF, banks[NH * t + h][:]) for t in range(TT) for h in range(NH)]
         sums[-1] = (last_t, HALF, NARROW, banks[-1][:, :NARROW])
         closing = (last_t, N - NARROW, NARROW, banks[0][:, :NARROW])
-
-        def warm_up(n, lhs):
-            for i in range(n):
-                nc.tensor.matmul_mx(
-                    out=banks[-1][:],
-                    lhsT=lhs.bitcast(FP4X4),
-                    lhsT_scale=zero_scales[:, :P],
-                    rhs=zero_codes[:].bitcast(FP8X4),
-                    rhs_scale=zero_scales[:],
-                    start=True,
-                    stop=True,
-                )
-
-        warm_up(WARM_EARLY, zero_codes[:, : P // 2])
 
         def mx_pass(lhs, lhs_scale, a, one, start, stop):
             n0, width, acc = one[1:]
@@ -168,9 +145,6 @@ def tile_mix_xres_tm_mul_kernel(tc, x4_words, x4_scales, xr, w4_words, w4_scales
         interleave(nc.vector.tensor_copy, 0, P, P + hp)
         quantize(0, 0, P)
         quantize(0, P, 2 * P)
-        late = sbuf("late", [P, hp], U32)
-        nc.vector.tensor_copy(late[:].bitcast(I32), zero_codes[:, :hp].bitcast(I32))
-        warm_up(WARM_LATE, late[:])
         interleave(nc.vector.tensor_copy, 0, 2 * P, 2 * P + hp)
         interleave(nc.scalar.copy, 0, 2 * P + hp, 3 * P)
         interleave(nc.scalar.copy, 0, 3 * P + hp, T)

from contextlib import ExitStack

import concourse.mybir as mybir

K, N, T = 2048, 1024, 512
FLOPS = 2 * 2 * K * N * T

F32 = mybir.dt.float32
BF16 = mybir.dt.bfloat16
U32 = mybir.dt.uint32
I32 = mybir.dt.int32
U8 = mybir.dt.uint8
FP8X4 = mybir.dt.float8_e4m3fn_x4
FP4X4 = mybir.dt.float4_e2m1fn_x4

P = 128
A = K // 512
TT = T // P
NH = 2
HALF = N // NH
NARROW = 256
VCOLS = 256


def tile_mix_xres_tm_mul_kernel(tc, x4_words, x4_scales, xr, w4_words, w4_scales, g, out):
    nc = tc.nc
    with ExitStack() as ctx:
        keep = ctx.enter_context(tc.tile_pool(name="keep", bufs=1))
        psum = ctx.enter_context(tc.psum_pool(name="psum", bufs=1))
        ctx.enter_context(tc.manual_schedule())

        last_t = TT - 1
        last_a = A - 1

        def sbuf(name, shape, dtype):
            return keep.tile(shape, dtype, name=name, align_bytes=256)

        def flat(tile, dtype):
            return tile[:].rearrange("p a n -> p (a n)").bitcast(dtype)

        xw01 = sbuf("xw01", [P, 2, 2 * T], U8)
        xw23 = sbuf("xw23", [P, 2, 2 * T], U8)
        ww = [sbuf("ww%d" % a, [P, 1, 2 * N], U8) for a in range(A)]
        split = T // 2
        raw_head = sbuf("raw_head", [P, 4, split], F32)
        raw_tail = sbuf("raw_tail", [P, 4, T - split], F32)
        raw = [None] + [sbuf("raw%d" % a, [P, 4, T], F32) for a in range(1, A)]
        g_sb = [sbuf("g%d" % t, [P, N], F32) for t in range(TT)]
        xs = sbuf("xs", [P, A, T], U8)
        ws01 = sbuf("ws01", [P, 2, N], U8)
        ws23 = sbuf("ws23", [P, 2, N], U8)

        for plane in (ws01, xs):
            nc.vector.memset(flat(plane, I32), 0)
        nc.vector.memset(flat(ws23, I32), 0)

        def load_scales(plane, dram, a0, a1):
            n4 = dram.shape[2] // 4
            for r in range(4):
                nc.sync.dma_start(
                    out=flat(plane, I32)[r:P:32, :].rearrange("q (a n) -> q a n", n=n4),
                    in_=dram.bitcast(I32)[a0:a1, r:16:4, :].rearrange("a q n -> q a n"),
                )

        def load_words(tile, dram, a0, a1):
            nc.sync.dma_start(out=tile[:], in_=dram[a0:a1].rearrange("a p n -> p a n"))

        def load_xr(tile, a, t0, t1):
            rows = xr[512 * a : 512 * (a + 1), t0:t1]
            nc.sync.dma_start(out=tile[:], in_=rows.rearrange("(p j) t -> p j t", j=4))

        load_xr(raw_head, 0, 0, split)
        load_scales(ws01, w4_scales, 0, 2)
        load_words(ww[0], w4_words, 0, 1)
        load_xr(raw_tail, 0, split, T)
        load_words(xw01, x4_words, 0, 2)
        load_scales(xs, x4_scales, 0, A)
        load_words(ww[1], w4_words, 1, 2)
        load_xr(raw[1], 1, 0, T)
        load_scales(ws23, w4_scales, 2, A)
        load_words(xw23, x4_words, 2, A)
        load_words(ww[2], w4_words, 2, 3)
        load_xr(raw[2], 2, 0, T)
        load_xr(raw[last_a], last_a, 0, T)
        load_words(ww[last_a], w4_words, last_a, A)
        for t in range(TT):
            nc.sync.dma_start(out=g_sb[t][:], in_=g[P * t : P * (t + 1), :])

        banks = [psum.tile([P, HALF], F32, name="bank%d" % i) for i in range(TT * NH)]

        sums = [(t, HALF * h, HALF, banks[NH * t + h][:]) for t in range(TT) for h in range(NH)]
        sums[-1] = (last_t, HALF, NARROW, banks[-1][:, :NARROW])
        closing = (last_t, N - NARROW, NARROW, banks[0][:, :NARROW])

        def mx_pass(lhs, lhs_scale, a, one, start, stop):
            n0, width, acc = one[1:]
            plane = ws01 if a < 2 else ws23
            nc.tensor.matmul_mx(
                out=acc,
                lhsT=lhs,
                lhsT_scale=lhs_scale,
                rhs=ww[a][:, 0, 2 * n0 : 2 * (n0 + width)].bitcast(FP4X4),
                rhs_scale=plane[:, a % 2, n0 : n0 + width],
                start=start,
                stop=stop,
            )

        def x4_pass(a, one, start=False):
            t = one[0]
            words = xw01 if a < 2 else xw23
            lhs = words[:, a % 2, 2 * P * t : 2 * P * (t + 1)].bitcast(FP4X4)
            mx_pass(lhs, xs[:, a, P * t : P * (t + 1)], a, one, start, False)

        xb = [sbuf("xb%d" % a, [P, T, 4], BF16) for a in range(A)]
        codes = [sbuf("codes%d" % a, [P, T], U32) for a in range(A)]
        scales = [sbuf("scales%d" % a, [P, T], U8) for a in range(A)]

        def xr_pass(a, one, start=False):
            t = one[0]
            lhs = codes[a][:, P * t : P * (t + 1)].bitcast(FP8X4)
            mx_pass(lhs, scales[a][:, P * t : P * (t + 1)], a, one, start, a == last_a)

        def interleave(copy, a, t0, t1):
            if a > 0:
                source = raw[a][:, :, t0:t1]
            elif t0 < split:
                source = raw_head[:, :, t0:t1]
            else:
                source = raw_tail[:, :, t0 - split : t1 - split]
            copy(
                xb[a][:, t0:t1, :].rearrange("p (c i) j -> p c j i", i=4),
                source.rearrange("p j (c i) -> p c j i", i=4),
            )

        def quantize(a, t0, t1):
            nc.vector.quantize_mx(
                out=codes[a][:, t0:t1].bitcast(FP8X4),
                scales=scales[a][:, t0:t1],
                in_=xb[a][:, t0:t1, :].rearrange("p t j -> p (t j)"),
            )

        hp = P // 2
        interleave(nc.vector.tensor_copy, 0, 0, P)
        interleave(nc.scalar.copy, 0, P + hp, 2 * P)
        interleave(nc.vector.tensor_copy, 0, P, P + hp)
        quantize(0, 0, P)
        quantize(0, P, 2 * P)
        interleave(nc.vector.tensor_copy, 0, 2 * P, 2 * P + hp)
        interleave(nc.scalar.copy, 0, 2 * P + hp, 3 * P)
        interleave(nc.scalar.copy, 0, 3 * P + hp, T)
        interleave(nc.vector.tensor_copy, 0, 3 * P, 3 * P + hp)
        quantize(0, 2 * P, 3 * P)
        quantize(0, 3 * P, T)
        for a in range(1, last_a):
            interleave(nc.vector.tensor_copy, a, 0, P)
            interleave(nc.scalar.copy, a, VCOLS, T)
            interleave(nc.vector.tensor_copy, a, P, VCOLS)
            quantize(a, 0, P)
            quantize(a, P, VCOLS)
            quantize(a, VCOLS, T)
        interleave(nc.vector.tensor_copy, last_a, 0, hp)
        interleave(nc.scalar.copy, last_a, hp, P)
        interleave(nc.scalar.copy, last_a, 2 * P, 3 * P)
        interleave(nc.vector.tensor_copy, last_a, P, P + hp)
        quantize(last_a, 0, P)
        interleave(nc.vector.tensor_copy, last_a, P + hp, 2 * P)
        interleave(nc.vector.tensor_copy, last_a, 3 * P, 3 * P + hp)
        quantize(last_a, P, 2 * P)
        interleave(nc.vector.tensor_copy, last_a, 3 * P + hp, T)
        quantize(last_a, 2 * P, 3 * P)
        quantize(last_a, 3 * P, T)

        for one in sums:
            xr_pass(0, one, start=True)
        for one in sums:
            x4_pass(0, one)
        for a in range(1, last_a):
            for one in sums:
                x4_pass(a, one)
            for one in sums[: NH * last_t]:
                xr_pass(a, one)

        results = [sbuf("result%d" % t, [P, N], F32) for t in range(TT)]

        def times_g(one):
            t, n0, width, acc = one
            nc.vector.tensor_tensor(
                out=results[t][:, n0 : n0 + width],
                in0=acc,
                in1=g_sb[t][:, n0 : n0 + width],
                op=mybir.AluOpType.mult,
            )

        def store(t, n0, n1):
            nc.sync.dma_start(out=out[P * t : P * (t + 1), n0:n1], in_=results[t][:, n0:n1])

        for i, one in enumerate(sums):
            t = one[0]
            x4_pass(last_a, one)
            for a in range(1 if t == last_t else last_a, A):
                xr_pass(a, one)
            times_g(one)
            if i % NH == NH - 1:
                store(t, 0, one[1] + one[2])
        for a in range(A):
            x4_pass(a, closing, start=a == 0)
        for a in range(A):
            xr_pass(a, closing)
        times_g(closing)
        store(last_t, N - NARROW, N)
